import numpy as np
import ml_dtypes


def mxq(x, axis, fmt="e4m3"):
    dtype, down = {"e4m3": (ml_dtypes.float8_e4m3fn, 7), "e5m2": (ml_dtypes.float8_e5m2, 14)}[fmt]
    v = np.moveaxis(np.asarray(x, np.float32).astype(ml_dtypes.bfloat16).astype(np.float64), axis, -1)
    blocks = v.reshape(v.shape[:-1] + (-1, 32))
    amax = np.abs(blocks).max(-1, keepdims=True)
    byte = np.maximum(np.where(amax > 0, np.frexp(amax)[1] - 1 + 127, 0) - down, 1)
    scale = np.exp2(byte - 127.0)
    codes = (blocks / scale).astype(np.float32).astype(dtype).astype(np.float64)
    return np.moveaxis((codes * scale).reshape(v.shape), -1, axis)


WIDE = False


def mx_kscale(k):
    if not WIDE:
        return np.ones(k)
    levels = np.array([10, -10, 5, -5, 0])
    if k % 512:
        return np.exp2(np.random.permutation(np.resize(levels, k // 32))).repeat(32)
    a = np.empty((k // 512, 16))
    for p in range(k // 512):
        a[p, :8] = np.random.permutation(np.resize(levels, 8))
        for g in range(8):
            far = levels[np.abs(levels - a[p, g]) >= 10]
            a[p, g + 8] = far[np.random.randint(len(far))]
    return np.exp2(a.ravel()).repeat(32)


def f64(x):
    return np.asarray(x).astype(np.float64)


def striped(idx):
    return np.tile(idx.reshape(-1, 16).T, (8, 1)).astype(np.uint16)


def unstriped(offs):
    return offs[:16].T.reshape(-1).astype(np.int64)


def striped8(idx):
    return np.concatenate([x.reshape(-1, 16).T for x in idx]).astype(np.uint16)


def runs(offs, k):
    lists = np.stack([offs[16 * r : 16 * r + 16].T.reshape(-1) for r in range(8)]).astype(np.int64)
    return lists[np.arange(k) % 512 // 64]


def pack_weight(w):
    k, n = w.shape
    w = f64(np.asarray(w, np.float32).astype(ml_dtypes.bfloat16)).reshape(k // 32, 32, n)
    amax = np.abs(w).max(1)
    byte = np.clip(np.where(amax > 0, np.frexp(amax)[1] - 1 + 127 - 7, 1), 1, 254)
    scaled = (w * np.exp2(127.0 - byte)[:, None, :]).reshape(k, n).astype(np.float32)
    words = np.ascontiguousarray(scaled.reshape(k // 512, 128, 4, n).transpose(0, 1, 3, 2)).astype(ml_dtypes.float8_e4m3fn).view(np.uint8)
    return words, np.ascontiguousarray(byte.astype(np.uint8).reshape(k // 512, 16, n))


def unpack_weight(words, scales):
    g, p, n, _ = words.shape
    vals = np.ascontiguousarray(words).view(ml_dtypes.float8_e4m3fn).astype(np.float64) * np.repeat(np.exp2(scales.astype(np.float64) - 127.0), 8, axis=1)[..., None]
    return vals.transpose(0, 1, 3, 2).reshape(g * 512, n)


K, T, S, V, G, H, W = 512, 1024, 512, 512, 2048, 512, 256


def setup_inputs():
    n = np.random.standard_normal
    s = mx_kscale(K)[:, None]
    u = mx_kscale(S)
    packed_xT = pack_weight(n((K, T)) * s)
    packed_dT = pack_weight(n((K, G)) / s)
    perm = np.stack([np.random.permutation(V) for _ in range(8)])
    return {
        "x_words": packed_xT[0],
        "x_scales": packed_xT[1],
        "d_words": packed_dT[0],
        "d_scales": packed_dT[1],
        "w1": (n((K, H)) / np.sqrt(K) / s).astype(np.float32),
        "ga": (np.random.uniform(0.5, 1.5, (H, 1)) * u[:, None]).astype(np.float32),
        "gb": (np.random.uniform(0.5, 1.5, (H, 1)) / u[:, None]).astype(np.float32),
        "offs": striped(np.random.permutation(T)[:S]),
        "k1": striped8(np.random.randint(0, G, (8, H))),
        "two": striped(np.random.permutation(T)[:V]),
        "n1": striped8(np.stack([np.random.permutation(S) for _ in range(8)])),
        "n2": striped8(np.stack([np.random.permutation(S) for _ in range(8)])),
        "n3": striped8(perm[:, :W]),
        "n4": striped8(perm[:, W:]),
        "n5": striped8(np.stack([np.random.permutation(V) for _ in range(8)])),
        "n6": striped8(np.stack([np.random.permutation(V) for _ in range(8)])),
        "n7": striped8(np.stack([np.random.permutation(V) for _ in range(8)])),
    }


def reference(x_words, x_scales, d_words, d_scales, w1, ga, gb, offs, k1, two, n1, n2, n3, n4, n5, n6, n7):
    d_k1 = unpack_weight(d_words, d_scales)[np.arange(K)[:, None], runs(k1, K)]
    xq = unpack_weight(x_words, x_scales)[:, unstriped(offs)]
    a = 0.0625 * (d_k1.T @ xq)
    z = f64(ga) * (np.maximum(a[np.arange(H)[:, None], runs(n1, H)], a[np.arange(H)[:, None], runs(n2, H)]) - (0.75 * a))
    x_two = unpack_weight(x_words, x_scales)[:, unstriped(two)]
    b = mxq(f64(w1), 0, "e4m3").T @ x_two
    pa = b[np.arange(H)[:, None], runs(n3, H)]
    pb = b[np.arange(H)[:, None], runs(n4, H)]
    ra = pa - (0.5 * pb)
    ds = b.copy()
    ds[np.arange(H)[:, None], runs(n4, H)] = ra
    z2 = f64(gb) * (ds - (0.5 * (ds[np.arange(H)[:, None], runs(n5, H)])))
    s = 0.0625 * ((mxq(z, 0, "e4m3").T @ mxq(z2, 0, "e4m3")))
    st = np.maximum(s, s[np.arange(S)[:, None], runs(n6, S)])
    return np.minimum(st, st[np.arange(S)[:, None], runs(n7, S)])

@@ -1,0 +1,265 @@
+from contextlib import ExitStack
+
+import concourse.mybir as mybir
+from concourse.masks import make_identity
+
+FLOPS = 3 * 2 * 512 * 512 * 512
+
+F32 = mybir.dt.float32
+BF16 = mybir.dt.bfloat16
+I32 = mybir.dt.int32
+U32 = mybir.dt.uint32
+U16 = mybir.dt.uint16
+U8 = mybir.dt.uint8
+FP8X4 = mybir.dt.float8_e4m3fn_x4
+ALU = mybir.AluOpType
+ACT = mybir.ActivationFunctionType
+
+P = 128
+PACK = 4
+N = 512
+TOKENS = 1024
+CODEWORDS = 2048
+PAIRS = 256
+PIECES = ((0, 256), (256, 384), (384, 512))
+
+
+def tile_picked_ckqoverfolddhopmn_none_p_kernel(
+    tc, x_words, x_scales, d_words, d_scales, w1, ga, gb, offs, k1, two, n1, n2, n3, n4, n5, n6, n7, out
+):
+    nc = tc.nc
+    with ExitStack() as ctx:
+        lists = ctx.enter_context(tc.tile_pool(name="lists", bufs=1))
+        sb = ctx.enter_context(tc.tile_pool(name="sb", bufs=1))
+        psum = ctx.enter_context(tc.psum_pool(name="psum", bufs=1))
+
+        def load_list(src, name):
+            tile = lists.tile(list(src.shape), U16, name=name)
+            nc.sync.dma_start(tile[:], src)
+            return tile
+
+        def gather(dst, window, offsets):
+            nc.vector.tensor_copy(dst, window[:].indirect(offsets))
+
+        def mx_product(dst, lhs_words, lhs_bytes, rhs_words, rhs_bytes):
+            nc.tensor.matmul_mx(
+                out=dst, lhsT=lhs_words.bitcast(FP8X4), lhsT_scale=lhs_bytes,
+                rhs=rhs_words.bitcast(FP8X4), rhs_scale=rhs_bytes, start=True, stop=True,
+            )
+
+        d_byte_table = sb.tile([P, CODEWORDS], U8, name="d_byte_table")
+        x_byte_table = sb.tile([P, TOKENS], U8, name="x_byte_table")
+        nc.vector.memset(d_byte_table[:].bitcast(I32), 0)
+        nc.vector.memset(x_byte_table[:].bitcast(I32), 0)
+        k1_t = load_list(k1, "k1_t")
+        for e in range(2):
+            nc.sync.dma_start(d_byte_table[e:P:16, :].bitcast(I32), d_scales[0, e:16:2, :].bitcast(I32))
+        offs_t = load_list(offs, "offs_t")
+        for q in range(4):
+            nc.sync.dma_start(x_byte_table[32 * q : 32 * q + 4, :].bitcast(I32), x_scales[0, 4 * q : 4 * q + 4, :].bitcast(I32))
+        x_word_table = sb.tile([P, TOKENS], U32, name="x_word_table")
+        nc.sync.dma_start(x_word_table[:].bitcast(I32), x_words[0].rearrange("p n t -> p (n t)").bitcast(I32))
+        d_word_table = sb.tile([P, CODEWORDS], U32, name="d_word_table")
+        nc.sync.dma_start(d_word_table[:].bitcast(I32), d_words[0].rearrange("p n t -> p (n t)").bitcast(I32))
+        two_t = load_list(two, "two_t")
+        ga_t = sb.tile([P, PACK], F32, name="ga_t")
+        nc.sync.dma_start(ga_t[:], ga.rearrange("(p t) o -> p (t o)", t=PACK))
+        n1_t = load_list(n1, "n1_t")
+        n2_t = load_list(n2, "n2_t")
+        gb_t = sb.tile([P, PACK], F32, name="gb_t")
+        nc.sync.dma_start(gb_t[:], gb.rearrange("(p t) o -> p (t o)", t=PACK))
+        w_raw = sb.tile([P, PACK, N], F32, name="w_raw")
+        nc.sync.dma_start(w_raw[:], w1.rearrange("(p j) c -> p j c", j=PACK))
+        n3_t = load_list(n3, "n3_t")
+        n4_t = load_list(n4, "n4_t")
+        n5_t = load_list(n5, "n5_t")
+        n6_t = load_list(n6, "n6_t")
+        n7_t = load_list(n7, "n7_t")
+
+        identity = sb.tile([P, P], F32, name="identity")
+        make_identity(nc, identity[:])
+
+        d_bytes_picked = sb.tile([P, N], U8, name="d_bytes_picked")
+        gather(d_bytes_picked[:], d_byte_table, k1_t[:])
+        d_bytes_dealt = sb.tile([P, N], U8, name="d_bytes_dealt")
+        nc.vector.tensor_copy(
+            d_bytes_dealt[:].rearrange("p (t g i) -> p g t i", t=PACK, i=16),
+            d_bytes_picked[:].rearrange("p (g i t) -> p g t i", t=PACK, i=16),
+        )
+        d_bytes = sb.tile([P, N], U8, name="d_bytes", align_bytes=64)
+        nc.vector.tensor_copy(d_bytes[:].bitcast(I32), d_bytes_dealt[:].bitcast(I32))
+        for e in range(2):
+            nc.scalar.dma_start(d_bytes[2 + e : P : 32, :].bitcast(I32), d_bytes_dealt[16 + e : P : 32, :].bitcast(I32))
+
+        xa_bytes = sb.tile([P, N], U8, name="xa_bytes", align_bytes=64)
+        gather(xa_bytes[:], x_byte_table, offs_t[:])
+        xa_words = sb.tile([P, N], U32, name="xa_words", align_bytes=64)
+        gather(xa_words[:], x_word_table, offs_t[:])
+        d_words_picked = sb.tile([P, N], U32, name="d_words_picked")
+        gather(d_words_picked[:], d_word_table, k1_t[:])
+        d_codes = sb.tile([P, N], U32, name="d_codes", align_bytes=64)
+        nc.vector.tensor_copy(
+            d_codes[:].rearrange("p (t g i) -> p g t i", t=PACK, i=4),
+            d_words_picked[:].rearrange("p (g i t) -> p g t i", t=PACK, i=4),
+        )
+
+        a_factor = sb.tile([P, PACK], F32, name="a_factor")
+        nc.scalar.activation(a_factor[:], ga_t[:], ACT.Abs, scale=0.0625)
+        c_factor = sb.tile([P, PACK], F32, name="c_factor")
+        nc.scalar.activation(c_factor[:], a_factor[:], ACT.Copy, scale=-0.75)
+        ga_sign = sb.tile([P, PACK], F32, name="ga_sign")
+        nc.scalar.activation(ga_sign[:], ga_t[:], ACT.Sign)
+        b_factor = sb.tile([P, PACK], F32, name="b_factor")
+        nc.gpsimd.tensor_tensor(b_factor[:], gb_t[:], ga_sign[:], ALU.mult)
+
+        a_win = []
+        for t in range(PACK):
+            cols = slice(P * t, P * (t + 1))
+            acc = psum.tile([P, N], F32, name="acc", tag="acc", bufs=2)
+            mx_product(acc[:], d_codes[:, cols], d_bytes[:, cols], xa_words[:], xa_bytes[:])
+            win = sb.tile([P, 2 * N], F32, name="a_win%d" % t)
+            nc.scalar.activation(win[:, :N], acc[:], ACT.Copy, scale=a_factor[:, t : t + 1])
+            nc.scalar.activation(win[:, N:], acc[:], ACT.Copy, scale=c_factor[:, t : t + 1])
+            a_win.append(win)
+
+        xb_bytes = sb.tile([P, N], U8, name="xb_bytes", align_bytes=64)
+        gather(xb_bytes[:], x_byte_table, two_t[:])
+        xb_words = sb.tile([P, N], U32, name="xb_words", align_bytes=64)
+        gather(xb_words[:], x_word_table, two_t[:])
+
+        zt_acc = [psum.tile([P, PACK, P], F32, name="zt_acc", tag="wide", bufs=4) for j in range(PACK)]
+        pair = [sb.tile([P, 2 * N], F32, name="pair%d" % t) for t in range(PACK)]
+
+        def first_neighbour(t):
+            gather(pair[t][:, :N], a_win[t], n1_t[:])
+
+        def second_neighbour(t):
+            nc.vector.tensor_tensor(pair[t][:, N:], a_win[t][:].indirect(n2_t[:]), pair[t][:, :N], ALU.subtract)
+            excess = sb.tile([P, N], F32, name="excess", bufs=2)
+            nc.scalar.activation(excess[:], pair[t][:, N:], ACT.Relu)
+            for j in range(PACK):
+                cols = slice(P * j, P * (j + 1))
+                terms = (pair[t][:, :N], a_win[t][:, N:], excess[:])
+                for n, term in enumerate(terms):
+                    nc.tensor.matmul(
+                        zt_acc[j][:, t, :], lhsT=term[:, cols], rhs=identity[:], is_transpose=True,
+                        start=(n == 0), stop=(n == len(terms) - 1),
+                    )
+
+        first_neighbour(0)
+        for t in range(PACK):
+            if t + 1 < PACK:
+                first_neighbour(t + 1)
+            second_neighbour(t)
+
+        w_grouped = sb.tile([P, N, PACK], BF16, name="w_grouped", align_bytes=64)
+        for h in range(4):
+            ms = slice(32 * h, 32 * (h + 1))
+            nc.scalar.copy(
+                w_grouped[:].rearrange("p (t m) j -> p m t j", t=PACK)[:, ms],
+                w_raw[:].rearrange("p j (m t) -> p m t j", t=PACK)[:, ms],
+            )
+        w_codes = sb.tile([P, N], U32, name="w_codes", align_bytes=64)
+        w_bytes = sb.tile([P, N], U8, name="w_bytes", align_bytes=64)
+        nc.vector.quantize_mx(out=w_codes[:].bitcast(FP8X4), scales=w_bytes[:], in_=w_grouped[:].rearrange("p c j -> p (c j)"))
+
+        b_win = []
+        for t in range(PACK):
+            cols = slice(P * t, P * (t + 1))
+            acc = psum.tile([P, N], F32, name="acc", tag="acc", bufs=2)
+            mx_product(acc[:], w_codes[:, cols], w_bytes[:, cols], xb_words[:], xb_bytes[:])
+            win = sb.tile([P, N], F32, name="b_win%d" % t)
+            nc.scalar.activation(win[:], acc[:], ACT.Copy, scale=b_factor[:, t : t + 1])
+            b_win.append(win)
+
+        z_grouped = sb.tile([P, N, PACK], BF16, name="z_grouped", align_bytes=64)
+        z_pairs = z_grouped[:].rearrange("p c j -> p (c j)").bitcast(F32).rearrange("p (t j m u) -> p j t m u", t=PACK, j=PACK, u=2)
+        for j in range(PACK):
+            zt = sb.tile([P, 2, P, 2], BF16, name="zt", bufs=2)
+            nc.scalar.copy(zt[:], zt_acc[j][:].rearrange("i (u e) p -> i u p e", e=2))
+            zt_words = zt[:].rearrange("i u p e -> i (u p e)").bitcast(F32)
+            back = psum.tile([P, 2, P], F32, name="back", tag="back", bufs=2)
+            for u in range(2):
+                nc.tensor.transpose(back[:, u, :], zt_words[:, P * u : P * (u + 1)], identity[:])
+            nc.scalar.copy(z_pairs[:, j], back[:].rearrange("p u (m t) -> p t m u", t=PACK))
+
+        doubled = []
+
+        def pick_pairs(t):
+            pa = sb.tile([P, PAIRS], F32, name="pa", bufs=2)
+            gather(pa[:], b_win[t], n3_t[:])
+            pb = sb.tile([P, PAIRS], F32, name="pb", bufs=2)
+            nc.vector.tensor_scalar(pb[:], b_win[t][:].indirect(n4_t[:]), -0.5, 0.0, ALU.mult, ALU.add)
+            return pa, pb
+
+        def put_back(t, pa, pb):
+            nc.vector.tensor_tensor(b_win[t][:].indirect(n4_t[:]), pa[:], pb[:], ALU.add)
+            twice = sb.tile([P, N], F32, name="twice%d" % t)
+            nc.scalar.activation(twice[:], b_win[t][:], ACT.Copy, scale=2.0)
+            doubled.append(twice)
+
+        picked = pick_pairs(0)
+        for t in range(PACK):
+            ahead = pick_pairs(t + 1) if t + 1 < PACK else None
+            put_back(t, *picked)
+            picked = ahead
+
+        z_codes = sb.tile([P, N], U32, name="z_codes", align_bytes=64)
+        z_bytes = sb.tile([P, N], U8, name="z_bytes", align_bytes=64)
+        nc.vector.quantize_mx(out=z_codes[:].bitcast(FP8X4), scales=z_bytes[:], in_=z_grouped[:].rearrange("p c j -> p (c j)"))
+
+        s_acc = [psum.tile([P, N], F32, name="s_acc", tag="wide", bufs=4) for t in range(PACK)]
+        last_acc = [psum.tile([P, P], F32, name="last_acc", tag=tag, bufs=2) for tag in ("acc", "acc", "back", "back")]
+        grouped = []
+        for n, (lo, hi) in enumerate(PIECES):
+            width = hi - lo
+            diff = sb.tile([P, PACK, width], F32, name="diff%d" % n)
+            for t in range(PACK):
+                nc.vector.tensor_tensor(
+                    diff[:, t, :], b_win[t][:].indirect(n5_t[:, lo // 16 : hi // 16]), doubled[t][:, lo:hi], ALU.subtract
+                )
+            z2 = sb.tile([P, width, PACK], BF16, name="z2_%d" % n, align_bytes=64)
+            if n + 1 < len(PIECES):
+                nc.scalar.activation(z2[:], diff[:].rearrange("p t c -> p c t"), ACT.Copy, scale=-0.5)
+            else:
+                nc.vector.tensor_scalar(
+                    z2[:].rearrange("p (c i) t -> p c t i", i=4), diff[:].rearrange("p t (c i) -> p c t i", i=4),
+                    -0.5, None, ALU.mult,
+                )
+            grouped.append(z2)
+        for n, (lo, hi) in enumerate(PIECES):
+            width = hi - lo
+            codes = sb.tile([P, width], U32, name="z2_codes%d" % n, align_bytes=64)
+            scale_bytes = sb.tile([P, width], U8, name="z2_bytes%d" % n, align_bytes=64)
+            nc.vector.quantize_mx(out=codes[:].bitcast(FP8X4), scales=scale_bytes[:], in_=grouped[n][:].rearrange("p c j -> p (c j)"))
+            for t in range(PACK):
+                cols = slice(P * t, P * (t + 1))
+                dst = s_acc[t][:, lo:hi] if n + 1 < len(PIECES) else last_acc[t][:]
+                mx_product(dst, z_codes[:, cols], z_bytes[:, cols], codes[:], scale_bytes[:])
+        for t in range(PACK):
+            lo = PIECES[-1][0]
+            nc.scalar.activation(a_win[t][:, :lo], s_acc[t][:, :lo], ACT.Copy, scale=0.0625)
+            nc.scalar.activation(a_win[t][:, lo:N], last_acc[t][:], ACT.Copy, scale=0.0625)
+
+        out_rows = out.rearrange("(p t) v -> t p v", t=PACK)
+        hop6 = []
+        for t in range(PACK):
+            g = sb.tile([P, N], F32, name="hop6_%d" % t)
+            gather(g[:], a_win[t], n6_t[:])
+            hop6.append(g)
+            if t > 0:
+                nc.vector.tensor_tensor(pair[t - 1][:, :N], a_win[t - 1][:, :N], hop6[t - 1][:], ALU.max)
+        hop7 = []
+        for t in range(PACK):
+            g = sb.tile([P, N], F32, name="hop7_%d" % t)
+            gather(g[:], pair[t], n7_t[:])
+            hop7.append(g)
+            if t == 0:
+                nc.vector.tensor_tensor(pair[PACK - 1][:, :N], a_win[PACK - 1][:, :N], hop6[PACK - 1][:], ALU.max)
+            else:
+                res = sb.tile([P, N], F32, name="res%d" % (t - 1))
+                nc.vector.tensor_tensor(res[:], pair[t - 1][:, :N], hop7[t - 1][:], ALU.min)
+                nc.sync.dma_start(out_rows[t - 1], res[:])
+        res = sb.tile([P, N], F32, name="res_last")
+        nc.vector.tensor_tensor(res[:], pair[PACK - 1][:, :N], hop7[PACK - 1][:], ALU.min)
+        nc.sync.dma_start(out_rows[PACK - 1], res[:])

@@ -48,28 +48,38 @@ def tile_picked_ckqoverfolddhopmn_none_p_kernel(
             )
 
         d_byte_table = sb.tile([P, CODEWORDS], U8, name="d_byte_table")
-        x_byte_table = sb.tile([P, TOKENS], U8, name="x_byte_table")
         nc.vector.memset(d_byte_table[:].bitcast(I32), 0)
-        nc.vector.memset(x_byte_table[:].bitcast(I32), 0)
+        x_byte_table = sb.tile([P, TOKENS], U8, name="x_byte_table")
+        nc.vector.memset(x_byte_table[: P - 16, :].bitcast(I32), 0)
+        a_win = [sb.tile([P, 2 * N], F32, name="a_win%d" % t) for t in range(PACK)]
+        nc.vector.memset(a_win[0][:, N:], 0.0)
+        two_column = sb.tile([P, 1], F32, name="two_column", tag="two_then_doubled")
+        nc.scalar.activation(two_column[:], a_win[0][:, N : N + 1], ACT.Copy, bias=2.0)
+        gains = sb.tile([P, P], F32, name="gains")
+        nc.gpsimd.memset(gains[: P - 8, :], 0.0)
+        x_bytes = sb.tile([P, 2 * N], U8, name="x_bytes", align_bytes=64)
+        nc.gpsimd.memset(x_bytes[:].bitcast(I32), 0)
+
+        offs_t = load_list(offs, "offs_t")
+        nc.sync.dma_start(x_byte_table[P - 16 :, :].bitcast(I32), x_scales[0].bitcast(I32))
         k1_t = load_list(k1, "k1_t")
         for e in range(2):
             nc.sync.dma_start(d_byte_table[e:P:16, :].bitcast(I32), d_scales[0, e:16:2, :].bitcast(I32))
-        offs_t = load_list(offs, "offs_t")
-        for q in range(4):
-            nc.sync.dma_start(x_byte_table[32 * q : 32 * q + 4, :].bitcast(I32), x_scales[0, 4 * q : 4 * q + 4, :].bitcast(I32))
+        two_t = load_list(two, "two_t")
+        for n, gain in enumerate((ga, gb)):
+            first = P - 8 + PACK * n
+            nc.sync.dma_start(
+                gains[first : first + PACK, :].rearrange("t (b r) -> t b r", r=8),
+                gain.rearrange("(b t r) o -> t b (r o)", t=PACK, r=8),
+            )
         x_word_table = sb.tile([P, TOKENS], U32, name="x_word_table")
         nc.sync.dma_start(x_word_table[:].bitcast(I32), x_words[0].rearrange("p n t -> p (n t)").bitcast(I32))
         d_word_table = sb.tile([P, CODEWORDS], U32, name="d_word_table")
         nc.sync.dma_start(d_word_table[:].bitcast(I32), d_words[0].rearrange("p n t -> p (n t)").bitcast(I32))
-        two_t = load_list(two, "two_t")
-        ga_t = sb.tile([P, PACK], F32, name="ga_t")
-        nc.sync.dma_start(ga_t[:], ga.rearrange("(p t) o -> p (t o)", t=PACK))
+        w_raw = sb.tile([P, PACK, N], F32, name="w_raw", tag="w_then_excess")
+        nc.sync.dma_start(w_raw[:], w1.rearrange("(p j) c -> p j c", j=PACK))
         n1_t = load_list(n1, "n1_t")
         n2_t = load_list(n2, "n2_t")
-        gb_t = sb.tile([P, PACK], F32, name="gb_t")
-        nc.sync.dma_start(gb_t[:], gb.rearrange("(p t) o -> p (t o)", t=PACK))
-        w_raw = sb.tile([P, PACK, N], F32, name="w_raw")
-        nc.sync.dma_start(w_raw[:], w1.rearrange("(p j) c -> p j c", j=PACK))
         n3_t = load_list(n3, "n3_t")
         n4_t = load_list(n4, "n4_t")
         n5_t = load_list(n5, "n5_t")
@@ -79,146 +89,176 @@ def tile_picked_ckqoverfolddhopmn_none_p_kernel(
         identity = sb.tile([P, P], F32, name="identity")
         make_identity(nc, identity[:])
 
+        x_bytes_picked = sb.tile([P, 2 * N], U8, name="x_bytes_picked")
+        gather(x_bytes_picked[:, :N], x_byte_table, offs_t[:])
         d_bytes_picked = sb.tile([P, N], U8, name="d_bytes_picked")
         gather(d_bytes_picked[:], d_byte_table, k1_t[:])
-        d_bytes_dealt = sb.tile([P, N], U8, name="d_bytes_dealt")
-        nc.vector.tensor_copy(
-            d_bytes_dealt[:].rearrange("p (t g i) -> p g t i", t=PACK, i=16),
-            d_bytes_picked[:].rearrange("p (g i t) -> p g t i", t=PACK, i=16),
-        )
+        gather(x_bytes_picked[:, N:], x_byte_table, two_t[:])
         d_bytes = sb.tile([P, N], U8, name="d_bytes", align_bytes=64)
-        nc.vector.tensor_copy(d_bytes[:].bitcast(I32), d_bytes_dealt[:].bitcast(I32))
+        nc.vector.tensor_copy(
+            d_bytes[:].bitcast(I32).rearrange("p (t b w) -> p t b w", t=PACK, w=2),
+            d_bytes_picked[:].bitcast(I32).rearrange("p (b t w) -> p t b w", t=PACK, w=2),
+        )
+        for q in range(4):
+            first = P - 16 + 4 * q
+            nc.scalar.dma_start(x_bytes[32 * q : 32 * q + 4, :].bitcast(I32), x_bytes_picked[first : first + 4, :].bitcast(I32))
         for e in range(2):
-            nc.scalar.dma_start(d_bytes[2 + e : P : 32, :].bitcast(I32), d_bytes_dealt[16 + e : P : 32, :].bitcast(I32))
+            nc.scalar.dma_start(d_bytes[2 + e : P : 32, :].bitcast(I32), d_bytes[16 + e : P : 32, :].bitcast(I32))
 
-        xa_bytes = sb.tile([P, N], U8, name="xa_bytes", align_bytes=64)
-        gather(xa_bytes[:], x_byte_table, offs_t[:])
         xa_words = sb.tile([P, N], U32, name="xa_words", align_bytes=64)
         gather(xa_words[:], x_word_table, offs_t[:])
-        d_words_picked = sb.tile([P, N], U32, name="d_words_picked")
+        d_words_picked = sb.tile([P, N], U32, name="d_words_picked", tag="picked_words", align_bytes=64)
         gather(d_words_picked[:], d_word_table, k1_t[:])
         d_codes = sb.tile([P, N], U32, name="d_codes", align_bytes=64)
         nc.vector.tensor_copy(
-            d_codes[:].rearrange("p (t g i) -> p g t i", t=PACK, i=4),
-            d_words_picked[:].rearrange("p (g i t) -> p g t i", t=PACK, i=4),
+            d_codes[:].rearrange("p (t b r) -> p t b r", t=PACK, r=8),
+            d_words_picked[:].rearrange("p (b t r) -> p t b r", t=PACK, r=8),
         )
-
-        a_factor = sb.tile([P, PACK], F32, name="a_factor")
-        nc.scalar.activation(a_factor[:], ga_t[:], ACT.Abs, scale=0.0625)
-        c_factor = sb.tile([P, PACK], F32, name="c_factor")
-        nc.scalar.activation(c_factor[:], a_factor[:], ACT.Copy, scale=-0.75)
-        ga_sign = sb.tile([P, PACK], F32, name="ga_sign")
-        nc.scalar.activation(ga_sign[:], ga_t[:], ACT.Sign)
-        b_factor = sb.tile([P, PACK], F32, name="b_factor")
-        nc.gpsimd.tensor_tensor(b_factor[:], gb_t[:], ga_sign[:], ALU.mult)
-
-        a_win = []
-        for t in range(PACK):
-            cols = slice(P * t, P * (t + 1))
-            acc = psum.tile([P, N], F32, name="acc", tag="acc", bufs=2)
-            mx_product(acc[:], d_codes[:, cols], d_bytes[:, cols], xa_words[:], xa_bytes[:])
-            win = sb.tile([P, 2 * N], F32, name="a_win%d" % t)
-            nc.scalar.activation(win[:, :N], acc[:], ACT.Copy, scale=a_factor[:, t : t + 1])
-            nc.scalar.activation(win[:, N:], acc[:], ACT.Copy, scale=c_factor[:, t : t + 1])
-            a_win.append(win)
-
-        xb_bytes = sb.tile([P, N], U8, name="xb_bytes", align_bytes=64)
-        gather(xb_bytes[:], x_byte_table, two_t[:])
-        xb_words = sb.tile([P, N], U32, name="xb_words", align_bytes=64)
+        xb_words = sb.tile([P, N], U32, name="xb_words", tag="picked_words", align_bytes=64)
         gather(xb_words[:], x_word_table, two_t[:])
 
-        zt_acc = [psum.tile([P, PACK, P], F32, name="zt_acc", tag="wide", bufs=4) for j in range(PACK)]
-        pair = [sb.tile([P, 2 * N], F32, name="pair%d" % t) for t in range(PACK)]
+        gains_turned = psum.tile([P, P], F32, name="gains_turned", tag="back", bufs=2)
+        nc.tensor.transpose(gains_turned[:], gains[:], identity[:])
+        gains_t = sb.tile([P, 2 * PACK], F32, name="gains_t")
+        nc.scalar.copy(gains_t[:], gains_turned[:, P - 8 :])
+        ga_t = gains_t[:, :PACK]
+        gb_t = gains_t[:, PACK:]
+        pair = {t: sb.tile([P, 2 * N], F32, name="pair%d" % t, align_bytes=64) for t in range(PACK - 1)}
+        a_factor_first = sb.tile([P, 1], F32, name="a_factor_first")
+        a_factor = [a_factor_first[:]] + [pair[t][:, N : N + 1] for t in range(PACK - 1)]
+        for t in range(PACK):
+            nc.scalar.activation(a_factor[t], ga_t[:, t : t + 1], ACT.Abs, scale=0.0625)
+        c_size = sb.tile([P, PACK], F32, name="c_size")
+        nc.scalar.activation(c_size[:], ga_t, ACT.Abs, scale=0.75 * 0.0625)
+        c_factor = sb.tile([P, PACK], F32, name="c_factor")
+        nc.scalar.activation(c_factor[:], c_size[:], ACT.Copy, scale=-1.0)
+        ga_sign = sb.tile([P, PACK], F32, name="ga_sign")
+        nc.scalar.activation(ga_sign[:], ga_t, ACT.Sign)
+        b_factor_low = sb.tile([P, 2], F32, name="b_factor_low", tag="factor_then_pa")
+        b_factor_high = sb.tile([P, 2], F32, name="b_factor_high")
+        nc.gpsimd.tensor_tensor(b_factor_low[:], gb_t[:, :2], ga_sign[:, :2], ALU.mult)
+        nc.gpsimd.tensor_tensor(b_factor_high[:], gb_t[:, 2:], ga_sign[:, 2:], ALU.mult)
+        b_factor = [tile[:, n : n + 1] for tile in (b_factor_low, b_factor_high) for n in range(2)]
+
+        c_last = sb.tile([P, N], F32, name="c_last")
+        c_part = [a_win[t + 1][:, N:] for t in range(PACK - 1)] + [c_last[:]]
+
+        def product_a(t):
+            cols = slice(P * t, P * (t + 1))
+            acc = psum.tile([P, N], F32, name="acc", tag="acc", bufs=2)
+            mx_product(acc[:], d_codes[:, cols], d_bytes[:, cols], xa_words[:], x_bytes[:, :N])
+            nc.scalar.activation(a_win[t][:, :N], acc[:], ACT.Copy, scale=a_factor[t])
+            nc.scalar.activation(c_part[t], acc[:], ACT.Copy, scale=c_factor[:, t : t + 1])
+
+        product_a(0)
+        product_a(1)
+        w_grouped = sb.tile([P, N, PACK], BF16, name="w_grouped", tag="w_then_pair", align_bytes=64)
+        for h in range(4):
+            blocks = slice(4 * h, 4 * (h + 1))
+            nc.scalar.copy(
+                w_grouped[:].rearrange("p (t b r) j -> p b t r j", t=PACK, r=8)[:, blocks],
+                w_raw[:].rearrange("p j (b t r) -> p b t r j", t=PACK, r=8)[:, blocks],
+            )
+        product_a(2)
+        product_a(3)
 
         def first_neighbour(t):
             gather(pair[t][:, :N], a_win[t], n1_t[:])
 
         def second_neighbour(t):
             nc.vector.tensor_tensor(pair[t][:, N:], a_win[t][:].indirect(n2_t[:]), pair[t][:, :N], ALU.subtract)
-            excess = sb.tile([P, N], F32, name="excess", bufs=2)
-            nc.scalar.activation(excess[:], pair[t][:, N:], ACT.Relu)
-            for j in range(PACK):
-                cols = slice(P * j, P * (j + 1))
-                terms = (pair[t][:, :N], a_win[t][:, N:], excess[:])
-                for n, term in enumerate(terms):
-                    nc.tensor.matmul(
-                        zt_acc[j][:, t, :], lhsT=term[:, cols], rhs=identity[:], is_transpose=True,
-                        start=(n == 0), stop=(n == len(terms) - 1),
-                    )
 
         first_neighbour(0)
-        for t in range(PACK):
-            if t + 1 < PACK:
-                first_neighbour(t + 1)
-            second_neighbour(t)
+        first_neighbour(1)
+        second_neighbour(0)
+        first_neighbour(2)
+        second_neighbour(1)
 
-        w_grouped = sb.tile([P, N, PACK], BF16, name="w_grouped", align_bytes=64)
-        for h in range(4):
-            ms = slice(32 * h, 32 * (h + 1))
-            nc.scalar.copy(
-                w_grouped[:].rearrange("p (t m) j -> p m t j", t=PACK)[:, ms],
-                w_raw[:].rearrange("p j (m t) -> p m t j", t=PACK)[:, ms],
-            )
         w_codes = sb.tile([P, N], U32, name="w_codes", align_bytes=64)
         w_bytes = sb.tile([P, N], U8, name="w_bytes", align_bytes=64)
         nc.vector.quantize_mx(out=w_codes[:].bitcast(FP8X4), scales=w_bytes[:], in_=w_grouped[:].rearrange("p c j -> p (c j)"))
-
         b_win = []
         for t in range(PACK):
             cols = slice(P * t, P * (t + 1))
             acc = psum.tile([P, N], F32, name="acc", tag="acc", bufs=2)
-            mx_product(acc[:], w_codes[:, cols], w_bytes[:, cols], xb_words[:], xb_bytes[:])
+            mx_product(acc[:], w_codes[:, cols], w_bytes[:, cols], xb_words[:], x_bytes[:, N:])
             win = sb.tile([P, N], F32, name="b_win%d" % t)
-            nc.scalar.activation(win[:], acc[:], ACT.Copy, scale=b_factor[:, t : t + 1])
+            nc.scalar.activation(win[:], acc[:], ACT.Copy, scale=b_factor[t])
             b_win.append(win)
 
-        z_grouped = sb.tile([P, N, PACK], BF16, name="z_grouped", align_bytes=64)
-        z_pairs = z_grouped[:].rearrange("p c j -> p (c j)").bitcast(F32).rearrange("p (t j m u) -> p j t m u", t=PACK, j=PACK, u=2)
+        pair[PACK - 1] = sb.tile([P, 2 * N], F32, name="pair_last", tag="w_then_pair", align_bytes=64)
+        first_neighbour(3)
+        second_neighbour(2)
+        second_neighbour(3)
+
+        def add_transposed(dst, terms):
+            for n, term in enumerate(terms):
+                nc.tensor.matmul(dst, lhsT=term, rhs=identity[:], is_transpose=True, start=(n == 0), stop=(n == len(terms) - 1))
+
+        zt_acc = [psum.tile([P, PACK, P], F32, name="zt_acc", tag="wide", bufs=4) for j in range(PACK)]
+        excess = sb.tile([P, PACK, N], F32, name="excess", tag="w_then_excess")
+        for t in range(PACK):
+            nc.scalar.activation(excess[:, t, :], pair[t][:, N:], ACT.Relu)
+            for j in range(PACK):
+                cols = slice(P * j, P * (j + 1))
+                add_transposed(zt_acc[j][:, t, :], (pair[t][:, :N][:, cols], c_part[t][:, cols], excess[:, t, cols]))
+        z_grouped = sb.tile([P, PACK, P, PACK], BF16, name="z_grouped", align_bytes=64)
+        z_pairs = z_grouped[:].rearrange("p u m t -> p (u m t)").bitcast(F32).rearrange("p (u j m h) -> p j u m h", u=PACK, j=PACK, h=2)
         for j in range(PACK):
             zt = sb.tile([P, 2, P, 2], BF16, name="zt", bufs=2)
-            nc.scalar.copy(zt[:], zt_acc[j][:].rearrange("i (u e) p -> i u p e", e=2))
-            zt_words = zt[:].rearrange("i u p e -> i (u p e)").bitcast(F32)
+            nc.scalar.copy(zt[:], zt_acc[j][:].rearrange("i (h e) p -> i h p e", e=2))
+            zt_words = zt[:].rearrange("i h p e -> i (h p e)").bitcast(F32)
             back = psum.tile([P, 2, P], F32, name="back", tag="back", bufs=2)
-            for u in range(2):
-                nc.tensor.transpose(back[:, u, :], zt_words[:, P * u : P * (u + 1)], identity[:])
-            nc.scalar.copy(z_pairs[:, j], back[:].rearrange("p u (m t) -> p t m u", t=PACK))
+            for h in range(2):
+                nc.tensor.transpose(back[:, h, :], zt_words[:, P * h : P * (h + 1)], identity[:])
+            nc.scalar.copy(z_pairs[:, j], back[:].rearrange("p h (m u) -> p u m h", u=PACK))
 
-        doubled = []
+        wide_lo, wide_hi = PIECES[0]
+        doubled = {}
 
         def pick_pairs(t):
-            pa = sb.tile([P, PAIRS], F32, name="pa", bufs=2)
+            pa = sb.tile([P, PAIRS], F32, name="pa%d" % t, tag="factor_then_pa" if t == 0 else "pa%d" % t)
             gather(pa[:], b_win[t], n3_t[:])
-            pb = sb.tile([P, PAIRS], F32, name="pb", bufs=2)
+            pb = sb.tile([P, PAIRS], F32, name="pb%d" % t)
             nc.vector.tensor_scalar(pb[:], b_win[t][:].indirect(n4_t[:]), -0.5, 0.0, ALU.mult, ALU.add)
             return pa, pb
 
         def put_back(t, pa, pb):
             nc.vector.tensor_tensor(b_win[t][:].indirect(n4_t[:]), pa[:], pb[:], ALU.add)
-            twice = sb.tile([P, N], F32, name="twice%d" % t)
-            nc.scalar.activation(twice[:], b_win[t][:], ACT.Copy, scale=2.0)
-            doubled.append(twice)
+            twice = sb.tile([P, wide_hi - wide_lo], F32, name="twice%d" % t)
+            nc.scalar.activation(twice[:], b_win[t][:, wide_lo:wide_hi], ACT.Copy, scale=two_column[:] if t == PACK - 1 else 2.0)
+            doubled[0, t] = twice[:]
 
         picked = pick_pairs(0)
         for t in range(PACK):
             ahead = pick_pairs(t + 1) if t + 1 < PACK else None
             put_back(t, *picked)
             picked = ahead
+        doubled_rest = sb.tile([P, PACK, N - wide_hi], F32, name="doubled_rest", tag="two_then_doubled")
+        for n, (lo, hi) in list(enumerate(PIECES))[1:]:
+            for t in range(PACK):
+                doubled[n, t] = doubled_rest[:, t, lo - wide_hi : hi - wide_hi]
+                nc.scalar.activation(doubled[n, t], b_win[t][:, lo:hi], ACT.Copy, scale=2.0)
 
-        z_codes = sb.tile([P, N], U32, name="z_codes", align_bytes=64)
         z_bytes = sb.tile([P, N], U8, name="z_bytes", align_bytes=64)
-        nc.vector.quantize_mx(out=z_codes[:].bitcast(FP8X4), scales=z_bytes[:], in_=z_grouped[:].rearrange("p c j -> p (c j)"))
 
-        s_acc = [psum.tile([P, N], F32, name="s_acc", tag="wide", bufs=4) for t in range(PACK)]
-        last_acc = [psum.tile([P, P], F32, name="last_acc", tag=tag, bufs=2) for tag in ("acc", "acc", "back", "back")]
+        def quantise_z(lo, hi, codes):
+            nc.vector.quantize_mx(
+                out=codes.bitcast(FP8X4), scales=z_bytes[:, P * lo : P * hi], in_=z_grouped[:, lo:hi].rearrange("p u m t -> p (u m t)")
+            )
+
+        z_first = sb.tile([P, P], U32, name="z_first", align_bytes=64)
+        quantise_z(0, 1, z_first[:])
+
         grouped = []
         for n, (lo, hi) in enumerate(PIECES):
             width = hi - lo
             diff = sb.tile([P, PACK, width], F32, name="diff%d" % n)
             for t in range(PACK):
                 nc.vector.tensor_tensor(
-                    diff[:, t, :], b_win[t][:].indirect(n5_t[:, lo // 16 : hi // 16]), doubled[t][:, lo:hi], ALU.subtract
+                    diff[:, t, :], b_win[t][:].indirect(n5_t[:, lo // 16 : hi // 16]), doubled[n, t], ALU.subtract
                 )
-            z2 = sb.tile([P, width, PACK], BF16, name="z2_%d" % n, align_bytes=64)
+            z2 = sb.tile([P, width, PACK], BF16, name="z2_%d" % n, tag="z2_%d" % n, align_bytes=64)
             if n + 1 < len(PIECES):
                 nc.scalar.activation(z2[:], diff[:].rearrange("p t c -> p c t"), ACT.Copy, scale=-0.5)
             else:
@@ -227,39 +267,57 @@ def tile_picked_ckqoverfolddhopmn_none_p_kernel(
                     -0.5, None, ALU.mult,
                 )
             grouped.append(z2)
+        s_acc = [psum.tile([P, N], F32, name="s_acc", tag="wide", bufs=4) for t in range(PACK)]
+        last_acc = psum.tile([P, P], F32, name="last_acc", tag="acc", bufs=2)
+        z2_mx = []
         for n, (lo, hi) in enumerate(PIECES):
             width = hi - lo
             codes = sb.tile([P, width], U32, name="z2_codes%d" % n, align_bytes=64)
             scale_bytes = sb.tile([P, width], U8, name="z2_bytes%d" % n, align_bytes=64)
             nc.vector.quantize_mx(out=codes[:].bitcast(FP8X4), scales=scale_bytes[:], in_=grouped[n][:].rearrange("p c j -> p (c j)"))
-            for t in range(PACK):
-                cols = slice(P * t, P * (t + 1))
-                dst = s_acc[t][:, lo:hi] if n + 1 < len(PIECES) else last_acc[t][:]
-                mx_product(dst, z_codes[:, cols], z_bytes[:, cols], codes[:], scale_bytes[:])
-        for t in range(PACK):
-            lo = PIECES[-1][0]
-            nc.scalar.activation(a_win[t][:, :lo], s_acc[t][:, :lo], ACT.Copy, scale=0.0625)
-            nc.scalar.activation(a_win[t][:, lo:N], last_acc[t][:], ACT.Copy, scale=0.0625)
+            z2_mx.append((codes, scale_bytes))
+            dst = s_acc[0][:, lo:hi] if n + 1 < len(PIECES) else last_acc[:]
+            mx_product(dst, z_first[:], z_bytes[:, :P], codes[:], scale_bytes[:])
+        last_lo = PIECES[-1][0]
+        nc.scalar.activation(a_win[0][:, :last_lo], s_acc[0][:, :last_lo], ACT.Copy, scale=0.0625)
+        nc.scalar.activation(a_win[0][:, last_lo:N], last_acc[:], ACT.Copy, scale=0.0625)
+        z_others = sb.tile([P, (PACK - 1) * P], U32, name="z_others", tag="z2_%d" % (len(PIECES) - 1), align_bytes=64)
+        quantise_z(1, 2, z_others[:, :P])
+        quantise_z(2, 4, z_others[:, P:])
+        sixteenth = pair[0][:, :1]
+        nc.gpsimd.memset(sixteenth, 0.0625)
+        for t in range(1, PACK):
+            for (lo, hi), (codes, scale_bytes) in zip(PIECES, z2_mx):
+                mx_product(s_acc[t][:, lo:hi], z_others[:, P * (t - 1) : P * t], z_bytes[:, P * t : P * (t + 1)], codes[:], scale_bytes[:])
+            nc.scalar.activation(a_win[t][:, :N], s_acc[t][:], ACT.Copy, scale=sixteenth if t == 1 else 0.0625)
 
         out_rows = out.rearrange("(p t) v -> t p v", t=PACK)
         hop6 = []
+
+        def larger(t):
+            nc.vector.tensor_tensor(pair[t][:, :N], a_win[t][:, :N], hop6[t][:], ALU.max)
+
         for t in range(PACK):
             g = sb.tile([P, N], F32, name="hop6_%d" % t)
             gather(g[:], a_win[t], n6_t[:])
             hop6.append(g)
             if t > 0:
-                nc.vector.tensor_tensor(pair[t - 1][:, :N], a_win[t - 1][:, :N], hop6[t - 1][:], ALU.max)
+                larger(t - 1)
+        steps = [(t, 0, N) for t in range(PACK - 1)] + [(PACK - 1, 0, N // 2), (PACK - 1, N // 2, N)]
         hop7 = []
-        for t in range(PACK):
-            g = sb.tile([P, N], F32, name="hop7_%d" % t)
-            gather(g[:], pair[t], n7_t[:])
+
+        def smaller(n):
+            t, lo, hi = steps[n]
+            res = sb.tile([P, hi - lo], F32, name="res%d" % n)
+            nc.vector.tensor_tensor(res[:], pair[t][:, lo:hi], hop7[n][:], ALU.min)
+            nc.sync.dma_start(out_rows[t][:, lo:hi], res[:])
+
+        for n, (t, lo, hi) in enumerate(steps):
+            g = sb.tile([P, hi - lo], F32, name="hop7_%d" % n)
+            gather(g[:], pair[t], n7_t[:, lo // 16 : hi // 16])
             hop7.append(g)
-            if t == 0:
-                nc.vector.tensor_tensor(pair[PACK - 1][:, :N], a_win[PACK - 1][:, :N], hop6[PACK - 1][:], ALU.max)
+            if n == 0:
+                larger(PACK - 1)
             else:
-                res = sb.tile([P, N], F32, name="res%d" % (t - 1))
-                nc.vector.tensor_tensor(res[:], pair[t - 1][:, :N], hop7[t - 1][:], ALU.min)
-                nc.sync.dma_start(out_rows[t - 1], res[:])
-        res = sb.tile([P, N], F32, name="res_last")
-        nc.vector.tensor_tensor(res[:], pair[PACK - 1][:, :N], hop7[PACK - 1][:], ALU.min)
-        nc.sync.dma_start(out_rows[PACK - 1], res[:])
+                smaller(n - 1)
+        smaller(len(steps) - 1)

@@ -50,30 +50,29 @@ def tile_picked_ckqoverfolddhopmn_none_p_kernel(
         d_byte_table = sb.tile([P, CODEWORDS], U8, name="d_byte_table")
         nc.vector.memset(d_byte_table[:].bitcast(I32), 0)
         x_byte_table = sb.tile([P, TOKENS], U8, name="x_byte_table")
-        nc.vector.memset(x_byte_table[: P - 16, :].bitcast(I32), 0)
+        nc.vector.memset(x_byte_table[:].bitcast(I32), 0)
         a_win = [sb.tile([P, 2 * N], F32, name="a_win%d" % t) for t in range(PACK)]
         nc.vector.memset(a_win[0][:, N:], 0.0)
         two_column = sb.tile([P, 1], F32, name="two_column", tag="two_then_doubled")
         nc.scalar.activation(two_column[:], a_win[0][:, N : N + 1], ACT.Copy, bias=2.0)
         gains = sb.tile([P, P], F32, name="gains")
         nc.gpsimd.memset(gains[: P - 8, :], 0.0)
-        x_bytes = sb.tile([P, 2 * N], U8, name="x_bytes", align_bytes=64)
-        nc.gpsimd.memset(x_bytes[:].bitcast(I32), 0)
 
-        offs_t = load_list(offs, "offs_t")
-        nc.sync.dma_start(x_byte_table[P - 16 :, :].bitcast(I32), x_scales[0].bitcast(I32))
         k1_t = load_list(k1, "k1_t")
         for e in range(2):
             nc.sync.dma_start(d_byte_table[e:P:16, :].bitcast(I32), d_scales[0, e:16:2, :].bitcast(I32))
-        two_t = load_list(two, "two_t")
+        offs_t = load_list(offs, "offs_t")
+        for q in range(4):
+            nc.sync.dma_start(x_byte_table[32 * q : 32 * q + 4, :].bitcast(I32), x_scales[0, 4 * q : 4 * q + 4, :].bitcast(I32))
+        x_word_table = sb.tile([P, TOKENS], U32, name="x_word_table")
+        nc.sync.dma_start(x_word_table[:].bitcast(I32), x_words[0].rearrange("p n t -> p (n t)").bitcast(I32))
         for n, gain in enumerate((ga, gb)):
             first = P - 8 + PACK * n
             nc.sync.dma_start(
                 gains[first : first + PACK, :].rearrange("t (b r) -> t b r", r=8),
                 gain.rearrange("(b t r) o -> t b (r o)", t=PACK, r=8),
             )
-        x_word_table = sb.tile([P, TOKENS], U32, name="x_word_table")
-        nc.sync.dma_start(x_word_table[:].bitcast(I32), x_words[0].rearrange("p n t -> p (n t)").bitcast(I32))
+        two_t = load_list(two, "two_t")
         d_word_table = sb.tile([P, CODEWORDS], U32, name="d_word_table")
         nc.sync.dma_start(d_word_table[:].bitcast(I32), d_words[0].rearrange("p n t -> p (n t)").bitcast(I32))
         w_raw = sb.tile([P, PACK, N], F32, name="w_raw", tag="w_then_excess")
@@ -89,24 +88,21 @@ def tile_picked_ckqoverfolddhopmn_none_p_kernel(
         identity = sb.tile([P, P], F32, name="identity")
         make_identity(nc, identity[:])
 
-        x_bytes_picked = sb.tile([P, 2 * N], U8, name="x_bytes_picked")
-        gather(x_bytes_picked[:, :N], x_byte_table, offs_t[:])
         d_bytes_picked = sb.tile([P, N], U8, name="d_bytes_picked")
         gather(d_bytes_picked[:], d_byte_table, k1_t[:])
-        gather(x_bytes_picked[:, N:], x_byte_table, two_t[:])
+        x_bytes = sb.tile([P, 2 * N], U8, name="x_bytes", align_bytes=64)
+        gather(x_bytes[:, :N], x_byte_table, offs_t[:])
         d_bytes = sb.tile([P, N], U8, name="d_bytes", align_bytes=64)
         nc.vector.tensor_copy(
             d_bytes[:].bitcast(I32).rearrange("p (t b w) -> p t b w", t=PACK, w=2),
             d_bytes_picked[:].bitcast(I32).rearrange("p (b t w) -> p t b w", t=PACK, w=2),
         )
-        for q in range(4):
-            first = P - 16 + 4 * q
-            nc.scalar.dma_start(x_bytes[32 * q : 32 * q + 4, :].bitcast(I32), x_bytes_picked[first : first + 4, :].bitcast(I32))
         for e in range(2):
             nc.scalar.dma_start(d_bytes[2 + e : P : 32, :].bitcast(I32), d_bytes[16 + e : P : 32, :].bitcast(I32))
 
         xa_words = sb.tile([P, N], U32, name="xa_words", align_bytes=64)
         gather(xa_words[:], x_word_table, offs_t[:])
+        gather(x_bytes[:, N:], x_byte_table, two_t[:])
         d_words_picked = sb.tile([P, N], U32, name="d_words_picked", tag="picked_words", align_bytes=64)
         gather(d_words_picked[:], d_word_table, k1_t[:])
         d_codes = sb.tile([P, N], U32, name="d_codes", align_bytes=64)
@@ -136,8 +132,6 @@ def tile_picked_ckqoverfolddhopmn_none_p_kernel(
         nc.scalar.activation(ga_sign[:], ga_t, ACT.Sign)
         b_factor_low = sb.tile([P, 2], F32, name="b_factor_low", tag="factor_then_pa")
         b_factor_high = sb.tile([P, 2], F32, name="b_factor_high")
-        nc.gpsimd.tensor_tensor(b_factor_low[:], gb_t[:, :2], ga_sign[:, :2], ALU.mult)
-        nc.gpsimd.tensor_tensor(b_factor_high[:], gb_t[:, 2:], ga_sign[:, 2:], ALU.mult)
         b_factor = [tile[:, n : n + 1] for tile in (b_factor_low, b_factor_high) for n in range(2)]
 
         c_last = sb.tile([P, N], F32, name="c_last")
@@ -159,6 +153,8 @@ def tile_picked_ckqoverfolddhopmn_none_p_kernel(
                 w_grouped[:].rearrange("p (t b r) j -> p b t r j", t=PACK, r=8)[:, blocks],
                 w_raw[:].rearrange("p j (b t r) -> p b t r j", t=PACK, r=8)[:, blocks],
             )
+        for t in range(PACK):
+            nc.scalar.activation(b_factor[t], gb_t[:, t : t + 1], ACT.Copy, scale=ga_sign[:, t : t + 1])
         product_a(2)
         product_a(3)
 
@@ -285,39 +281,71 @@ def tile_picked_ckqoverfolddhopmn_none_p_kernel(
         quantise_z(1, 2, z_others[:, :P])
         quantise_z(2, 4, z_others[:, P:])
         sixteenth = pair[0][:, :1]
-        nc.gpsimd.memset(sixteenth, 0.0625)
+        nc.scalar.activation(sixteenth, a_win[0][:, N : N + 1], ACT.Copy, bias=0.0625)
         for t in range(1, PACK):
             for (lo, hi), (codes, scale_bytes) in zip(PIECES, z2_mx):
                 mx_product(s_acc[t][:, lo:hi], z_others[:, P * (t - 1) : P * t], z_bytes[:, P * t : P * (t + 1)], codes[:], scale_bytes[:])
+
+        def empty_s(t):
             nc.scalar.activation(a_win[t][:, :N], s_acc[t][:], ACT.Copy, scale=sixteenth if t == 1 else 0.0625)
 
         out_rows = out.rearrange("(p t) v -> t p v", t=PACK)
-        hop6 = []
+        hop6 = [sb.tile([P, N], F32, name="hop6_%d" % t) for t in range(PACK)]
+        hop7 = [sb.tile([P, N], F32, name="hop7_%d" % t) for t in range(PACK)]
+        res = [sb.tile([P, N], F32, name="res%d" % t) for t in range(PACK)]
+        negated = {}
+
+        def fetch6(t):
+            gather(hop6[t][:], a_win[t], n6_t[:])
 
         def larger(t):
             nc.vector.tensor_tensor(pair[t][:, :N], a_win[t][:, :N], hop6[t][:], ALU.max)
 
-        for t in range(PACK):
-            g = sb.tile([P, N], F32, name="hop6_%d" % t)
-            gather(g[:], a_win[t], n6_t[:])
-            hop6.append(g)
-            if t > 0:
-                larger(t - 1)
-        steps = [(t, 0, N) for t in range(PACK - 1)] + [(PACK - 1, 0, N // 2), (PACK - 1, N // 2, N)]
-        hop7 = []
+        def fetch7(t, lo=0, hi=N):
+            gather(hop7[t][:, lo:hi], pair[t], n7_t[:, lo // 16 : hi // 16])
 
-        def smaller(n):
-            t, lo, hi = steps[n]
-            res = sb.tile([P, hi - lo], F32, name="res%d" % n)
-            nc.vector.tensor_tensor(res[:], pair[t][:, lo:hi], hop7[n][:], ALU.min)
-            nc.sync.dma_start(out_rows[t][:, lo:hi], res[:])
+        def smaller(t, lo=0, hi=N):
+            nc.vector.tensor_tensor(res[t][:, lo:hi], pair[t][:, lo:hi], hop7[t][:, lo:hi], ALU.min)
+            nc.sync.dma_start(out_rows[t][:, lo:hi], res[t][:, lo:hi])
 
-        for n, (t, lo, hi) in enumerate(steps):
-            g = sb.tile([P, hi - lo], F32, name="hop7_%d" % n)
-            gather(g[:], pair[t], n7_t[:, lo // 16 : hi // 16])
-            hop7.append(g)
-            if n == 0:
-                larger(PACK - 1)
-            else:
-                smaller(n - 1)
-        smaller(len(steps) - 1)
+        def turn(dst, terms, func, scale, tag):
+            turned = psum.tile([P, N], F32, name="turned", tag=tag, bufs=2)
+            for j in range(PACK):
+                cols = slice(P * j, P * (j + 1))
+                add_transposed(turned[:, cols], [term[:, cols] for term in terms])
+            nc.scalar.activation(dst, turned[:], func, scale=scale)
+
+        def negate(t):
+            minus = sb.tile([P, N], F32, name="minus%d" % t)
+            nc.scalar.activation(minus[:], pair[t][:, :N], ACT.Copy, scale=-1.0)
+            minus_turned = sb.tile([P, N], F32, name="minus_turned%d" % t)
+            turn(minus_turned[:], [minus[:]], ACT.Copy, 1.0, "acc")
+            negated[t] = (minus, minus_turned)
+
+        def smaller_by_transposes(t):
+            minus, minus_turned = negated[t]
+            over = sb.tile([P, N], F32, name="over%d" % t)
+            turn(over[:], [minus[:], hop7[t][:]], ACT.Relu, -1.0, "back")
+            turn(res[t][:], [minus_turned[:], over[:]], ACT.Copy, -1.0, "acc")
+            nc.scalar.dma_start(out_rows[t], res[t][:])
+
+        for t in range(1, PACK):
+            empty_s(t)
+        fetch6(0)
+        fetch6(1)
+        for t in range(2):
+            larger(t)
+            negate(t)
+        for t in range(2):
+            fetch7(t)
+            smaller_by_transposes(t)
+        fetch6(2)
+        fetch6(3)
+        larger(2)
+        larger(3)
+        fetch7(2)
+        fetch7(3, 0, N // 2)
+        smaller(2)
+        fetch7(3, N // 2, N)
+        smaller(3, 0, N // 2)
+        smaller(3, N // 2, N)

@@ -21,7 +21,7 @@ N = 512
 TOKENS = 1024
 CODEWORDS = 2048
 PAIRS = 256
-PIECES = ((0, 256), (256, 384), (384, 512))
+PIECES = ((0, 256), (256, 512))
 
 
 def tile_picked_ckqoverfolddhopmn_none_p_kernel(
@@ -50,66 +50,72 @@ def tile_picked_ckqoverfolddhopmn_none_p_kernel(
         d_byte_table = sb.tile([P, CODEWORDS], U8, name="d_byte_table")
         nc.vector.memset(d_byte_table[:].bitcast(I32), 0)
         x_byte_table = sb.tile([P, TOKENS], U8, name="x_byte_table")
-        nc.vector.memset(x_byte_table[:].bitcast(I32), 0)
+        nc.vector.memset(x_byte_table[: P - 16, :].bitcast(I32), 0)
         a_win = [sb.tile([P, 2 * N], F32, name="a_win%d" % t) for t in range(PACK)]
         nc.vector.memset(a_win[0][:, N:], 0.0)
-        two_column = sb.tile([P, 1], F32, name="two_column", tag="two_then_doubled")
+        two_column = sb.tile([P, 1], F32, name="two_column", tag="two_then_doubled", align_bytes=64)
         nc.scalar.activation(two_column[:], a_win[0][:, N : N + 1], ACT.Copy, bias=2.0)
         gains = sb.tile([P, P], F32, name="gains")
         nc.gpsimd.memset(gains[: P - 8, :], 0.0)
+        x_bytes = sb.tile([P, 2 * N], U8, name="x_bytes", align_bytes=64)
+        nc.gpsimd.memset(x_bytes[:].bitcast(I32), 0)
 
+        offs_t = load_list(offs, "offs_t")
+        nc.sync.dma_start(x_byte_table[P - 16 :, :].bitcast(I32), x_scales[0].bitcast(I32))
         k1_t = load_list(k1, "k1_t")
         for e in range(2):
             nc.sync.dma_start(d_byte_table[e:P:16, :].bitcast(I32), d_scales[0, e:16:2, :].bitcast(I32))
-        offs_t = load_list(offs, "offs_t")
-        for q in range(4):
-            nc.sync.dma_start(x_byte_table[32 * q : 32 * q + 4, :].bitcast(I32), x_scales[0, 4 * q : 4 * q + 4, :].bitcast(I32))
-        x_word_table = sb.tile([P, TOKENS], U32, name="x_word_table")
-        nc.sync.dma_start(x_word_table[:].bitcast(I32), x_words[0].rearrange("p n t -> p (n t)").bitcast(I32))
+        two_t = load_list(two, "two_t")
         for n, gain in enumerate((ga, gb)):
             first = P - 8 + PACK * n
             nc.sync.dma_start(
                 gains[first : first + PACK, :].rearrange("t (b r) -> t b r", r=8),
                 gain.rearrange("(b t r) o -> t b (r o)", t=PACK, r=8),
             )
-        two_t = load_list(two, "two_t")
+        x_word_table = sb.tile([P, TOKENS], U32, name="x_word_table")
+        nc.sync.dma_start(x_word_table[:].bitcast(I32), x_words[0].rearrange("p n t -> p (n t)").bitcast(I32))
         d_word_table = sb.tile([P, CODEWORDS], U32, name="d_word_table")
         nc.sync.dma_start(d_word_table[:].bitcast(I32), d_words[0].rearrange("p n t -> p (n t)").bitcast(I32))
-        w_raw = sb.tile([P, PACK, N], F32, name="w_raw", tag="w_then_excess")
-        nc.sync.dma_start(w_raw[:], w1.rearrange("(p j) c -> p j c", j=PACK))
+
+        identity = sb.tile([P, P], F32, name="identity")
+        make_identity(nc, identity[:])
+
+        x_bytes_picked = sb.tile([P, 2 * N], U8, name="x_bytes_picked")
+        gather(x_bytes_picked[:, :N], x_byte_table, offs_t[:])
+        d_bytes_picked = sb.tile([P, N], U8, name="d_bytes_picked")
+        gather(d_bytes_picked[:], d_byte_table, k1_t[:])
+        gather(x_bytes_picked[:, N:], x_byte_table, two_t[:])
+        d_bytes = sb.tile([P, N], U8, name="d_bytes", align_bytes=64)
+        nc.vector.tensor_copy(
+            d_bytes[:].bitcast(I32).rearrange("p (t b w) -> p t b w", t=PACK, w=2),
+            d_bytes_picked[:].bitcast(I32).rearrange("p (b t w) -> p t b w", t=PACK, w=2),
+        )
+        for q in range(4):
+            first = P - 16 + 4 * q
+            nc.scalar.dma_start(x_bytes[32 * q : 32 * q + 4, :].bitcast(I32), x_bytes_picked[first : first + 4, :].bitcast(I32))
+        for e in range(2):
+            nc.sync.dma_start(d_bytes[2 + e : P : 32, :].bitcast(I32), d_bytes[16 + e : P : 32, :].bitcast(I32))
+
         n1_t = load_list(n1, "n1_t")
         n2_t = load_list(n2, "n2_t")
+        w_raw = sb.tile([P, PACK, N], F32, name="w_raw", tag="w_then_excess")
+        nc.sync.dma_start(w_raw[:], w1.rearrange("(p j) c -> p j c", j=PACK))
         n3_t = load_list(n3, "n3_t")
         n4_t = load_list(n4, "n4_t")
         n5_t = load_list(n5, "n5_t")
         n6_t = load_list(n6, "n6_t")
         n7_t = load_list(n7, "n7_t")
 
-        identity = sb.tile([P, P], F32, name="identity")
-        make_identity(nc, identity[:])
-
-        d_bytes_picked = sb.tile([P, N], U8, name="d_bytes_picked")
-        gather(d_bytes_picked[:], d_byte_table, k1_t[:])
-        x_bytes = sb.tile([P, 2 * N], U8, name="x_bytes", align_bytes=64)
-        gather(x_bytes[:, :N], x_byte_table, offs_t[:])
-        d_bytes = sb.tile([P, N], U8, name="d_bytes", align_bytes=64)
-        nc.vector.tensor_copy(
-            d_bytes[:].bitcast(I32).rearrange("p (t b w) -> p t b w", t=PACK, w=2),
-            d_bytes_picked[:].bitcast(I32).rearrange("p (b t w) -> p t b w", t=PACK, w=2),
-        )
-        for e in range(2):
-            nc.scalar.dma_start(d_bytes[2 + e : P : 32, :].bitcast(I32), d_bytes[16 + e : P : 32, :].bitcast(I32))
-
         xa_words = sb.tile([P, N], U32, name="xa_words", align_bytes=64)
         gather(xa_words[:], x_word_table, offs_t[:])
-        gather(x_bytes[:, N:], x_byte_table, two_t[:])
         d_words_picked = sb.tile([P, N], U32, name="d_words_picked", tag="picked_words", align_bytes=64)
         gather(d_words_picked[:], d_word_table, k1_t[:])
         d_codes = sb.tile([P, N], U32, name="d_codes", align_bytes=64)
-        nc.vector.tensor_copy(
-            d_codes[:].rearrange("p (t b r) -> p t b r", t=PACK, r=8),
-            d_words_picked[:].rearrange("p (b t r) -> p t b r", t=PACK, r=8),
-        )
+        for tiles in (slice(0, 1), slice(1, PACK)):
+            nc.vector.tensor_copy(
+                d_codes[:].rearrange("p (t b r) -> p t b r", t=PACK, r=8)[:, tiles],
+                d_words_picked[:].rearrange("p (b t r) -> p t b r", t=PACK, r=8)[:, tiles],
+            )
         xb_words = sb.tile([P, N], U32, name="xb_words", tag="picked_words", align_bytes=64)
         gather(xb_words[:], x_word_table, two_t[:])
 
@@ -126,26 +132,39 @@ def tile_picked_ckqoverfolddhopmn_none_p_kernel(
             nc.scalar.activation(a_factor[t], ga_t[:, t : t + 1], ACT.Abs, scale=0.0625)
         c_size = sb.tile([P, PACK], F32, name="c_size")
         nc.scalar.activation(c_size[:], ga_t, ACT.Abs, scale=0.75 * 0.0625)
-        c_factor = sb.tile([P, PACK], F32, name="c_factor")
-        nc.scalar.activation(c_factor[:], c_size[:], ACT.Copy, scale=-1.0)
+        c_factors = sb.tile([P, PACK], F32, name="c_factors")
+        nc.scalar.activation(c_factors[:], c_size[:], ACT.Copy, scale=-1.0)
+        c_factor_second = sb.tile([P, 1], F32, name="c_factor_second", tag="w_then_pair", align_bytes=64)
+        nc.scalar.activation(c_factor_second[:], c_size[:, 1:2], ACT.Copy, scale=-1.0)
+        c_factor = [c_factor_second[:] if t == 1 else c_factors[:, t : t + 1] for t in range(PACK)]
         ga_sign = sb.tile([P, PACK], F32, name="ga_sign")
         nc.scalar.activation(ga_sign[:], ga_t, ACT.Sign)
+        minus_half = sb.tile([P, 1], F32, name="minus_half", tag="half_then_codes", align_bytes=64)
+        nc.scalar.activation(minus_half[:], a_win[0][:, N : N + 1], ACT.Copy, bias=-0.5)
         b_factor_low = sb.tile([P, 2], F32, name="b_factor_low", tag="factor_then_pa")
-        b_factor_high = sb.tile([P, 2], F32, name="b_factor_high")
+        b_factor_high = sb.tile([P, 2], F32, name="b_factor_high", tag="factor_then_excess")
         b_factor = [tile[:, n : n + 1] for tile in (b_factor_low, b_factor_high) for n in range(2)]
 
         c_last = sb.tile([P, N], F32, name="c_last")
         c_part = [a_win[t + 1][:, N:] for t in range(PACK - 1)] + [c_last[:]]
 
-        def product_a(t):
+        def product_a(t, spans=((0, N),), tag="acc", bufs=2):
             cols = slice(P * t, P * (t + 1))
-            acc = psum.tile([P, N], F32, name="acc", tag="acc", bufs=2)
-            mx_product(acc[:], d_codes[:, cols], d_bytes[:, cols], xa_words[:], x_bytes[:, :N])
-            nc.scalar.activation(a_win[t][:, :N], acc[:], ACT.Copy, scale=a_factor[t])
-            nc.scalar.activation(c_part[t], acc[:], ACT.Copy, scale=c_factor[:, t : t + 1])
+            accs = []
+            for lo, hi in spans:
+                acc = psum.tile([P, hi - lo], F32, name="acc", tag=tag, bufs=bufs)
+                mx_product(acc[:], d_codes[:, cols], d_bytes[:, cols], xa_words[:, lo:hi], x_bytes[:, lo:hi])
+                nc.scalar.activation(a_win[t][:, lo:hi], acc[:], ACT.Copy, scale=a_factor[t])
+                accs.append((lo, hi, acc))
+            return accs
 
-        product_a(0)
-        product_a(1)
+        def own_share(t, accs):
+            for lo, hi, acc in accs:
+                nc.scalar.activation(c_part[t][:, lo:hi], acc[:], ACT.Copy, scale=c_factor[t])
+
+        own_share(0, product_a(0, ((0, N // 2), (N // 2, N)), "wide", 4))
+        own_share(1, product_a(1))
+        third = product_a(2)
         w_grouped = sb.tile([P, N, PACK], BF16, name="w_grouped", tag="w_then_pair", align_bytes=64)
         for h in range(4):
             blocks = slice(4 * h, 4 * (h + 1))
@@ -153,10 +172,10 @@ def tile_picked_ckqoverfolddhopmn_none_p_kernel(
                 w_grouped[:].rearrange("p (t b r) j -> p b t r j", t=PACK, r=8)[:, blocks],
                 w_raw[:].rearrange("p j (b t r) -> p b t r j", t=PACK, r=8)[:, blocks],
             )
+        own_share(2, third)
+        own_share(3, product_a(3, tag="wide", bufs=4))
         for t in range(PACK):
             nc.scalar.activation(b_factor[t], gb_t[:, t : t + 1], ACT.Copy, scale=ga_sign[:, t : t + 1])
-        product_a(2)
-        product_a(3)
 
         def first_neighbour(t):
             gather(pair[t][:, :N], a_win[t], n1_t[:])
@@ -192,12 +211,14 @@ def tile_picked_ckqoverfolddhopmn_none_p_kernel(
                 nc.tensor.matmul(dst, lhsT=term, rhs=identity[:], is_transpose=True, start=(n == 0), stop=(n == len(terms) - 1))
 
         zt_acc = [psum.tile([P, PACK, P], F32, name="zt_acc", tag="wide", bufs=4) for j in range(PACK)]
-        excess = sb.tile([P, PACK, N], F32, name="excess", tag="w_then_excess")
+        excess_low = sb.tile([P, 2, N], F32, name="excess_low", tag="w_then_excess")
+        excess_high = sb.tile([P, 2, N], F32, name="excess_high", tag="factor_then_excess")
+        excess = [tile[:, n, :] for tile in (excess_low, excess_high) for n in range(2)]
         for t in range(PACK):
-            nc.scalar.activation(excess[:, t, :], pair[t][:, N:], ACT.Relu)
+            nc.scalar.activation(excess[t], pair[t][:, N:], ACT.Relu)
             for j in range(PACK):
                 cols = slice(P * j, P * (j + 1))
-                add_transposed(zt_acc[j][:, t, :], (pair[t][:, :N][:, cols], c_part[t][:, cols], excess[:, t, cols]))
+                add_transposed(zt_acc[j][:, t, :], (pair[t][:, :N][:, cols], c_part[t][:, cols], excess[t][:, cols]))
         z_grouped = sb.tile([P, PACK, P, PACK], BF16, name="z_grouped", align_bytes=64)
         z_pairs = z_grouped[:].rearrange("p u m t -> p (u m t)").bitcast(F32).rearrange("p (u j m h) -> p j u m h", u=PACK, j=PACK, h=2)
         for j in range(PACK):
@@ -230,7 +251,7 @@ def tile_picked_ckqoverfolddhopmn_none_p_kernel(
             ahead = pick_pairs(t + 1) if t + 1 < PACK else None
             put_back(t, *picked)
             picked = ahead
-        doubled_rest = sb.tile([P, PACK, N - wide_hi], F32, name="doubled_rest", tag="two_then_doubled")
+        doubled_rest = sb.tile([P, PACK, N - wide_hi], F32, name="doubled_rest", tag="two_then_doubled", align_bytes=64)
         for n, (lo, hi) in list(enumerate(PIECES))[1:]:
             for t in range(PACK):
                 doubled[n, t] = doubled_rest[:, t, lo - wide_hi : hi - wide_hi]
@@ -246,45 +267,50 @@ def tile_picked_ckqoverfolddhopmn_none_p_kernel(
         z_first = sb.tile([P, P], U32, name="z_first", align_bytes=64)
         quantise_z(0, 1, z_first[:])
 
-        grouped = []
-        for n, (lo, hi) in enumerate(PIECES):
-            width = hi - lo
-            diff = sb.tile([P, PACK, width], F32, name="diff%d" % n)
+        first, last = range(len(PIECES))
+        width = N // 2
+        diff_first = sb.tile([P, PACK, width], F32, name="diff_first", tag="diff_then_z2", align_bytes=64)
+        diff_last = sb.tile([P, PACK, width], F32, name="diff_last")
+        diff = [diff_first, diff_last]
+        z2_codes = [sb.tile([P, width], U32, name="z2_codes%d" % n, align_bytes=64) for n in range(len(PIECES))]
+        z2_bytes = [sb.tile([P, width], U8, name="z2_bytes%d" % n, align_bytes=64) for n in range(len(PIECES))]
+        first_acc = [psum.tile([P, width], F32, name="first_acc", tag="acc", bufs=2) for n in range(len(PIECES))]
+        s_acc = {t: psum.tile([P, N], F32, name="s_acc", tag="wide", bufs=4) for t in range(1, PACK)}
+
+        def fetch5(n):
+            lo, hi = PIECES[n]
             for t in range(PACK):
                 nc.vector.tensor_tensor(
-                    diff[:, t, :], b_win[t][:].indirect(n5_t[:, lo // 16 : hi // 16]), doubled[n, t], ALU.subtract
+                    diff[n][:, t, :], b_win[t][:].indirect(n5_t[:, lo // 16 : hi // 16]), doubled[n, t], ALU.subtract
                 )
-            z2 = sb.tile([P, width, PACK], BF16, name="z2_%d" % n, tag="z2_%d" % n, align_bytes=64)
-            if n + 1 < len(PIECES):
-                nc.scalar.activation(z2[:], diff[:].rearrange("p t c -> p c t"), ACT.Copy, scale=-0.5)
-            else:
-                nc.vector.tensor_scalar(
-                    z2[:].rearrange("p (c i) t -> p c t i", i=4), diff[:].rearrange("p t (c i) -> p c t i", i=4),
-                    -0.5, None, ALU.mult,
-                )
-            grouped.append(z2)
-        s_acc = [psum.tile([P, N], F32, name="s_acc", tag="wide", bufs=4) for t in range(PACK)]
-        last_acc = psum.tile([P, P], F32, name="last_acc", tag="acc", bufs=2)
-        z2_mx = []
-        for n, (lo, hi) in enumerate(PIECES):
-            width = hi - lo
-            codes = sb.tile([P, width], U32, name="z2_codes%d" % n, align_bytes=64)
-            scale_bytes = sb.tile([P, width], U8, name="z2_bytes%d" % n, align_bytes=64)
-            nc.vector.quantize_mx(out=codes[:].bitcast(FP8X4), scales=scale_bytes[:], in_=grouped[n][:].rearrange("p c j -> p (c j)"))
-            z2_mx.append((codes, scale_bytes))
-            dst = s_acc[0][:, lo:hi] if n + 1 < len(PIECES) else last_acc[:]
-            mx_product(dst, z_first[:], z_bytes[:, :P], codes[:], scale_bytes[:])
-        last_lo = PIECES[-1][0]
-        nc.scalar.activation(a_win[0][:, :last_lo], s_acc[0][:, :last_lo], ACT.Copy, scale=0.0625)
-        nc.scalar.activation(a_win[0][:, last_lo:N], last_acc[:], ACT.Copy, scale=0.0625)
-        z_others = sb.tile([P, (PACK - 1) * P], U32, name="z_others", tag="z2_%d" % (len(PIECES) - 1), align_bytes=64)
-        quantise_z(1, 2, z_others[:, :P])
-        quantise_z(2, 4, z_others[:, P:])
+
+        def quantise_z2(n, rounded):
+            lo, hi = PIECES[n]
+            nc.vector.quantize_mx(out=z2_codes[n][:].bitcast(FP8X4), scales=z2_bytes[n][:], in_=rounded[:].rearrange("p c j -> p (c j)"))
+            mx_product(first_acc[n][:], z_first[:], z_bytes[:, :P], z2_codes[n][:], z2_bytes[n][:])
+            nc.scalar.activation(a_win[0][:, lo:hi], first_acc[n][:], ACT.Copy, scale=0.0625)
+
+        fetch5(first)
+        z2_first = sb.tile([P, width, PACK], BF16, name="z2_first", align_bytes=64)
+        nc.scalar.activation(z2_first[:], diff_first[:].rearrange("p t c -> p c t"), ACT.Copy, scale=minus_half[:])
+        fetch5(last)
+        quantise_z2(first, z2_first)
+        z2_last = sb.tile([P, width, PACK], BF16, name="z2_last", tag="diff_then_z2", align_bytes=64)
+        nc.vector.tensor_scalar(
+            z2_last[:].rearrange("p (c i) t -> p c t i", i=4), diff_last[:].rearrange("p t (c i) -> p c t i", i=4),
+            -0.5, None, ALU.mult,
+        )
+        quantise_z2(last, z2_last)
+        z_second = sb.tile([P, P], U32, name="z_second", tag="diff_then_z2", align_bytes=64)
+        quantise_z(1, 2, z_second[:])
+        z_others = sb.tile([P, 2 * P], U32, name="z_others", tag="half_then_codes", align_bytes=64)
+        quantise_z(2, 4, z_others[:])
+        z_codes = [z_first[:], z_second[:], z_others[:, :P], z_others[:, P:]]
         sixteenth = pair[0][:, :1]
         nc.scalar.activation(sixteenth, a_win[0][:, N : N + 1], ACT.Copy, bias=0.0625)
         for t in range(1, PACK):
-            for (lo, hi), (codes, scale_bytes) in zip(PIECES, z2_mx):
-                mx_product(s_acc[t][:, lo:hi], z_others[:, P * (t - 1) : P * t], z_bytes[:, P * t : P * (t + 1)], codes[:], scale_bytes[:])
+            for n, (lo, hi) in enumerate(PIECES):
+                mx_product(s_acc[t][:, lo:hi], z_codes[t], z_bytes[:, P * t : P * (t + 1)], z2_codes[n][:], z2_bytes[n][:])
 
         def empty_s(t):
             nc.scalar.activation(a_win[t][:, :N], s_acc[t][:], ACT.Copy, scale=sixteenth if t == 1 else 0.0625)

@@ -139,8 +139,6 @@ def tile_picked_ckqoverfolddhopmn_none_p_kernel(
         c_factor = [c_factor_second[:] if t == 1 else c_factors[:, t : t + 1] for t in range(PACK)]
         ga_sign = sb.tile([P, PACK], F32, name="ga_sign")
         nc.scalar.activation(ga_sign[:], ga_t, ACT.Sign)
-        minus_half = sb.tile([P, 1], F32, name="minus_half", tag="half_then_codes", align_bytes=64)
-        nc.scalar.activation(minus_half[:], a_win[0][:, N : N + 1], ACT.Copy, bias=-0.5)
         b_factor_low = sb.tile([P, 2], F32, name="b_factor_low", tag="factor_then_pa")
         b_factor_high = sb.tile([P, 2], F32, name="b_factor_high", tag="factor_then_excess")
         b_factor = [tile[:, n : n + 1] for tile in (b_factor_low, b_factor_high) for n in range(2)]
@@ -274,7 +272,6 @@ def tile_picked_ckqoverfolddhopmn_none_p_kernel(
         diff = [diff_first, diff_last]
         z2_codes = [sb.tile([P, width], U32, name="z2_codes%d" % n, align_bytes=64) for n in range(len(PIECES))]
         z2_bytes = [sb.tile([P, width], U8, name="z2_bytes%d" % n, align_bytes=64) for n in range(len(PIECES))]
-        first_acc = [psum.tile([P, width], F32, name="first_acc", tag="acc", bufs=2) for n in range(len(PIECES))]
         s_acc = {t: psum.tile([P, N], F32, name="s_acc", tag="wide", bufs=4) for t in range(1, PACK)}
 
         def fetch5(n):
@@ -284,28 +281,33 @@ def tile_picked_ckqoverfolddhopmn_none_p_kernel(
                     diff[n][:, t, :], b_win[t][:].indirect(n5_t[:, lo // 16 : hi // 16]), doubled[n, t], ALU.subtract
                 )
 
-        def quantise_z2(n, rounded):
-            lo, hi = PIECES[n]
-            nc.vector.quantize_mx(out=z2_codes[n][:].bitcast(FP8X4), scales=z2_bytes[n][:], in_=rounded[:].rearrange("p c j -> p (c j)"))
-            mx_product(first_acc[n][:], z_first[:], z_bytes[:, :P], z2_codes[n][:], z2_bytes[n][:])
-            nc.scalar.activation(a_win[0][:, lo:hi], first_acc[n][:], ACT.Copy, scale=0.0625)
+        def quantise_z2(n, rounded, cols, tag):
+            nc.vector.quantize_mx(
+                out=z2_codes[n][:, cols].bitcast(FP8X4), scales=z2_bytes[n][:, cols], in_=rounded[:, cols].rearrange("p c j -> p (c j)")
+            )
+            acc = psum.tile([P, cols.stop - cols.start], F32, name="first_acc", tag=tag, bufs=2)
+            mx_product(acc[:], z_first[:], z_bytes[:, :P], z2_codes[n][:, cols], z2_bytes[n][:, cols])
+            lo = PIECES[n][0]
+            nc.scalar.activation(a_win[0][:, lo + cols.start : lo + cols.stop], acc[:], ACT.Copy, scale=0.0625)
 
         fetch5(first)
         z2_first = sb.tile([P, width, PACK], BF16, name="z2_first", align_bytes=64)
-        nc.scalar.activation(z2_first[:], diff_first[:].rearrange("p t c -> p c t"), ACT.Copy, scale=minus_half[:])
+        nc.scalar.activation(z2_first[:], diff_first[:].rearrange("p t c -> p c t"), ACT.Copy, scale=-0.5)
         fetch5(last)
-        quantise_z2(first, z2_first)
+        quantise_z2(first, z2_first, slice(0, width), "acc")
         z2_last = sb.tile([P, width, PACK], BF16, name="z2_last", tag="diff_then_z2", align_bytes=64)
-        nc.vector.tensor_scalar(
-            z2_last[:].rearrange("p (c i) t -> p c t i", i=4), diff_last[:].rearrange("p t (c i) -> p c t i", i=4),
-            -0.5, None, ALU.mult,
-        )
-        quantise_z2(last, z2_last)
-        z_second = sb.tile([P, P], U32, name="z_second", tag="diff_then_z2", align_bytes=64)
-        quantise_z(1, 2, z_second[:])
-        z_others = sb.tile([P, 2 * P], U32, name="z_others", tag="half_then_codes", align_bytes=64)
-        quantise_z(2, 4, z_others[:])
-        z_codes = [z_first[:], z_second[:], z_others[:, :P], z_others[:, P:]]
+        halves = (slice(0, P), slice(P, width))
+        for cols in halves:
+            nc.vector.tensor_scalar(
+                z2_last[:, cols].rearrange("p (c i) t -> p c t i", i=4), diff_last[:, :, cols].rearrange("p t (c i) -> p c t i", i=4),
+                -0.5, None, ALU.mult,
+            )
+        for cols in halves:
+            quantise_z2(last, z2_last, cols, "back")
+        z_others = sb.tile([P, (PACK - 1) * P], U32, name="z_others", tag="diff_then_z2", align_bytes=64)
+        quantise_z(1, 2, z_others[:, :P])
+        quantise_z(2, 4, z_others[:, P:])
+        z_codes = [z_first[:]] + [z_others[:, P * n : P * (n + 1)] for n in range(PACK - 1)]
         sixteenth = pair[0][:, :1]
         nc.scalar.activation(sixteenth, a_win[0][:, N : N + 1], ACT.Copy, bias=0.0625)
         for t in range(1, PACK):

from contextlib import ExitStack

import concourse.mybir as mybir
from concourse.masks import make_identity

FLOPS = 3 * 2 * 512 * 512 * 512

F32 = mybir.dt.float32
BF16 = mybir.dt.bfloat16
I32 = mybir.dt.int32
U32 = mybir.dt.uint32
U16 = mybir.dt.uint16
U8 = mybir.dt.uint8
FP8X4 = mybir.dt.float8_e4m3fn_x4
ALU = mybir.AluOpType
ACT = mybir.ActivationFunctionType

P = 128
PACK = 4
N = 512
TOKENS = 1024
CODEWORDS = 2048
PAIRS = 256
PIECES = ((0, 256), (256, 512))


def tile_picked_ckqoverfolddhopmn_none_p_kernel(
    tc, x_words, x_scales, d_words, d_scales, w1, ga, gb, offs, k1, two, n1, n2, n3, n4, n5, n6, n7, out
):
    nc = tc.nc
    with ExitStack() as ctx:
        lists = ctx.enter_context(tc.tile_pool(name="lists", bufs=1))
        sb = ctx.enter_context(tc.tile_pool(name="sb", bufs=1))
        psum = ctx.enter_context(tc.psum_pool(name="psum", bufs=1))

        def load_list(src, name):
            tile = lists.tile(list(src.shape), U16, name=name)
            nc.sync.dma_start(tile[:], src)
            return tile

        def gather(dst, window, offsets):
            nc.vector.tensor_copy(dst, window[:].indirect(offsets))

        def mx_product(dst, lhs_words, lhs_bytes, rhs_words, rhs_bytes):
            nc.tensor.matmul_mx(
                out=dst, lhsT=lhs_words.bitcast(FP8X4), lhsT_scale=lhs_bytes,
                rhs=rhs_words.bitcast(FP8X4), rhs_scale=rhs_bytes, start=True, stop=True,
            )

        d_byte_table = sb.tile([P, CODEWORDS], U8, name="d_byte_table")
        nc.vector.memset(d_byte_table[:].bitcast(I32), 0)
        x_byte_table = sb.tile([P, TOKENS], U8, name="x_byte_table")
        nc.vector.memset(x_byte_table[: P - 16, :].bitcast(I32), 0)
        a_win = [sb.tile([P, 2 * N], F32, name="a_win%d" % t) for t in range(PACK)]
        nc.vector.memset(a_win[0][:, N:], 0.0)
        two_column = sb.tile([P, 1], F32, name="two_column", tag="two_then_doubled", align_bytes=64)
        nc.scalar.activation(two_column[:], a_win[0][:, N : N + 1], ACT.Copy, bias=2.0)
        gains = sb.tile([P, P], F32, name="gains")
        nc.gpsimd.memset(gains[: P - 8, :], 0.0)
        x_bytes = sb.tile([P, 2 * N], U8, name="x_bytes", align_bytes=64)
        nc.gpsimd.memset(x_bytes[:].bitcast(I32), 0)

        offs_t = load_list(offs, "offs_t")
        nc.sync.dma_start(x_byte_table[P - 16 :, :].bitcast(I32), x_scales[0].bitcast(I32))
        k1_t = load_list(k1, "k1_t")
        for e in range(2):
            nc.sync.dma_start(d_byte_table[e:P:16, :].bitcast(I32), d_scales[0, e:16:2, :].bitcast(I32))
        two_t = load_list(two, "two_t")
        for n, gain in enumerate((ga, gb)):
            first = P - 8 + PACK * n
            nc.sync.dma_start(
                gains[first : first + PACK, :].rearrange("t (b r) -> t b r", r=8),
                gain.rearrange("(b t r) o -> t b (r o)", t=PACK, r=8),
            )
        x_word_table = sb.tile([P, TOKENS], U32, name="x_word_table")
        nc.sync.dma_start(x_word_table[:].bitcast(I32), x_words[0].rearrange("p n t -> p (n t)").bitcast(I32))
        d_word_table = sb.tile([P, CODEWORDS], U32, name="d_word_table")
        nc.sync.dma_start(d_word_table[:].bitcast(I32), d_words[0].rearrange("p n t -> p (n t)").bitcast(I32))

        identity = sb.tile([P, P], F32, name="identity")
        make_identity(nc, identity[:])

        x_bytes_picked = sb.tile([P, 2 * N], U8, name="x_bytes_picked")
        gather(x_bytes_picked[:, :N], x_byte_table, offs_t[:])
        d_bytes_picked = sb.tile([P, N], U8, name="d_bytes_picked")
        gather(d_bytes_picked[:], d_byte_table, k1_t[:])
        gather(x_bytes_picked[:, N:], x_byte_table, two_t[:])
        d_bytes = sb.tile([P, N], U8, name="d_bytes", align_bytes=64)
        nc.vector.tensor_copy(
            d_bytes[:].bitcast(I32).rearrange("p (t b w) -> p t b w", t=PACK, w=2),
            d_bytes_picked[:].bitcast(I32).rearrange("p (b t w) -> p t b w", t=PACK, w=2),
        )
        for q in range(4):
            first = P - 16 + 4 * q
            nc.scalar.dma_start(x_bytes[32 * q : 32 * q + 4, :].bitcast(I32), x_bytes_picked[first : first + 4, :].bitcast(I32))
        for e in range(2):
            nc.sync.dma_start(d_bytes[2 + e : P : 32, :].bitcast(I32), d_bytes[16 + e : P : 32, :].bitcast(I32))

        n1_t = load_list(n1, "n1_t")
        n2_t = load_list(n2, "n2_t")
        w_raw = sb.tile([P, PACK, N], F32, name="w_raw", tag="w_then_excess")
        nc.sync.dma_start(w_raw[:], w1.rearrange("(p j) c -> p j c", j=PACK))
        n3_t = load_list(n3, "n3_t")
        n4_t = load_list(n4, "n4_t")
        n5_t = load_list(n5, "n5_t")
        n6_t = load_list(n6, "n6_t")
        n7_t = load_list(n7, "n7_t")

        xa_words = sb.tile([P, N], U32, name="xa_words", align_bytes=64)
        gather(xa_words[:], x_word_table, offs_t[:])
        d_words_picked = sb.tile([P, N], U32, name="d_words_picked", tag="picked_words", align_bytes=64)
        gather(d_words_picked[:], d_word_table, k1_t[:])
        d_codes = sb.tile([P, N], U32, name="d_codes", align_bytes=64)
        for tiles in (slice(0, 1), slice(1, PACK)):
            nc.vector.tensor_copy(
                d_codes[:].rearrange("p (t b r) -> p t b r", t=PACK, r=8)[:, tiles],
                d_words_picked[:].rearrange("p (b t r) -> p t b r", t=PACK, r=8)[:, tiles],
            )
        xb_words = sb.tile([P, N], U32, name="xb_words", tag="picked_words", align_bytes=64)
        gather(xb_words[:], x_word_table, two_t[:])

        gains_turned = psum.tile([P, P], F32, name="gains_turned", tag="back", bufs=2)
        nc.tensor.transpose(gains_turned[:], gains[:], identity[:])
        gains_t = sb.tile([P, 2 * PACK], F32, name="gains_t")
        nc.scalar.copy(gains_t[:], gains_turned[:, P - 8 :])
        ga_t = gains_t[:, :PACK]
        gb_t = gains_t[:, PACK:]
        pair = {t: sb.tile([P, 2 * N], F32, name="pair%d" % t, align_bytes=64) for t in range(PACK - 1)}
        a_factor_first = sb.tile([P, 1], F32, name="a_factor_first")
        a_factor = [a_factor_first[:]] + [pair[t][:, N : N + 1] for t in range(PACK - 1)]
        for t in range(PACK):
            nc.scalar.activation(a_factor[t], ga_t[:, t : t + 1], ACT.Abs, scale=0.0625)
        c_size = sb.tile([P, PACK], F32, name="c_size")
        nc.scalar.activation(c_size[:], ga_t, ACT.Abs, scale=0.75 * 0.0625)
        c_factors = sb.tile([P, PACK], F32, name="c_factors")
        nc.scalar.activation(c_factors[:], c_size[:], ACT.Copy, scale=-1.0)
        c_factor_second = sb.tile([P, 1], F32, name="c_factor_second", tag="w_then_pair", align_bytes=64)
        nc.scalar.activation(c_factor_second[:], c_size[:, 1:2], ACT.Copy, scale=-1.0)
        c_factor = [c_factor_second[:] if t == 1 else c_factors[:, t : t + 1] for t in range(PACK)]
        ga_sign = sb.tile([P, PACK], F32, name="ga_sign")
        nc.scalar.activation(ga_sign[:], ga_t, ACT.Sign)
        b_factor_low = sb.tile([P, 2], F32, name="b_factor_low", tag="factor_then_pa")
        b_factor_high = sb.tile([P, 2], F32, name="b_factor_high", tag="factor_then_excess")
        b_factor = [tile[:, n : n + 1] for tile in (b_factor_low, b_factor_high) for n in range(2)]

        c_last = sb.tile([P, N], F32, name="c_last")
        c_part = [a_win[t + 1][:, N:] for t in range(PACK - 1)] + [c_last[:]]

        def product_a(t, spans=((0, N),), tag="acc", bufs=2):
            cols = slice(P * t, P * (t + 1))
            accs = []
            for lo, hi in spans:
                acc = psum.tile([P, hi - lo], F32, name="acc", tag=tag, bufs=bufs)
                mx_product(acc[:], d_codes[:, cols], d_bytes[:, cols], xa_words[:, lo:hi], x_bytes[:, lo:hi])
                nc.scalar.activation(a_win[t][:, lo:hi], acc[:], ACT.Copy, scale=a_factor[t])
                accs.append((lo, hi, acc))
            return accs

        def own_share(t, accs):
            for lo, hi, acc in accs:
                nc.scalar.activation(c_part[t][:, lo:hi], acc[:], ACT.Copy, scale=c_factor[t])

        own_share(0, product_a(0, ((0, N // 2), (N // 2, N)), "wide", 4))
        own_share(1, product_a(1))
        third = product_a(2)
        w_grouped = sb.tile([P, N, PACK], BF16, name="w_grouped", tag="w_then_pair", align_bytes=64)
        for h in range(4):
            blocks = slice(4 * h, 4 * (h + 1))
            nc.scalar.copy(
                w_grouped[:].rearrange("p (t b r) j -> p b t r j", t=PACK, r=8)[:, blocks],
                w_raw[:].rearrange("p j (b t r) -> p b t r j", t=PACK, r=8)[:, blocks],
            )
        own_share(2, third)
        own_share(3, product_a(3, tag="wide", bufs=4))
        for t in range(PACK):
            nc.scalar.activation(b_factor[t], gb_t[:, t : t + 1], ACT.Copy, scale=ga_sign[:, t : t + 1])

        def first_neighbour(t):
            gather(pair[t][:, :N], a_win[t], n1_t[:])

        def second_neighbour(t):
            nc.vector.tensor_tensor(pair[t][:, N:], a_win[t][:].indirect(n2_t[:]), pair[t][:, :N], ALU.subtract)

        first_neighbour(0)
        first_neighbour(1)
        second_neighbour(0)
        first_neighbour(2)
        second_neighbour(1)

        w_codes = sb.tile([P, N], U32, name="w_codes", align_bytes=64)
        w_bytes = sb.tile([P, N], U8, name="w_bytes", align_bytes=64)
        nc.vector.quantize_mx(out=w_codes[:].bitcast(FP8X4), scales=w_bytes[:], in_=w_grouped[:].rearrange("p c j -> p (c j)"))
        b_win = []
        for t in range(PACK):
            cols = slice(P * t, P * (t + 1))
            acc = psum.tile([P, N], F32, name="acc", tag="acc", bufs=2)
            mx_product(acc[:], w_codes[:, cols], w_bytes[:, cols], xb_words[:], x_bytes[:, N:])
            win = sb.tile([P, N], F32, name="b_win%d" % t)
            nc.scalar.activation(win[:], acc[:], ACT.Copy, scale=b_factor[t])
            b_win.append(win)

        pair[PACK - 1] = sb.tile([P, 2 * N], F32, name="pair_last", tag="w_then_pair", align_bytes=64)
        first_neighbour(3)
        second_neighbour(2)
        second_neighbour(3)

        def add_transposed(dst, terms):
            for n, term in enumerate(terms):
                nc.tensor.matmul(dst, lhsT=term, rhs=identity[:], is_transpose=True, start=(n == 0), stop=(n == len(terms) - 1))

        zt_acc = [psum.tile([P, PACK, P], F32, name="zt_acc", tag="wide", bufs=4) for j in range(PACK)]
        excess_low = sb.tile([P, 2, N], F32, name="excess_low", tag="w_then_excess")
        excess_high = sb.tile([P, 2, N], F32, name="excess_high", tag="factor_then_excess")
        excess = [tile[:, n, :] for tile in (excess_low, excess_high) for n in range(2)]
        for t in range(PACK):
            nc.scalar.activation(excess[t], pair[t][:, N:], ACT.Relu)
            for j in range(PACK):
                cols = slice(P * j, P * (j + 1))
                add_transposed(zt_acc[j][:, t, :], (pair[t][:, :N][:, cols], c_part[t][:, cols], excess[t][:, cols]))
        z_grouped = sb.tile([P, PACK, P, PACK], BF16, name="z_grouped", align_bytes=64)
        z_pairs = z_grouped[:].rearrange("p u m t -> p (u m t)").bitcast(F32).rearrange("p (u j m h) -> p j u m h", u=PACK, j=PACK, h=2)
        for j in range(PACK):
            zt = sb.tile([P, 2, P, 2], BF16, name="zt", bufs=2)
            nc.scalar.copy(zt[:], zt_acc[j][:].rearrange("i (h e) p -> i h p e", e=2))
            zt_words = zt[:].rearrange("i h p e -> i (h p e)").bitcast(F32)
            back = psum.tile([P, 2, P], F32, name="back", tag="back", bufs=2)
            for h in range(2):
                nc.tensor.transpose(back[:, h, :], zt_words[:, P * h : P * (h + 1)], identity[:])
            nc.scalar.copy(z_pairs[:, j], back[:].rearrange("p h (m u) -> p u m h", u=PACK))

        wide_lo, wide_hi = PIECES[0]
        doubled = {}

        def pick_pairs(t):
            pa = sb.tile([P, PAIRS], F32, name="pa%d" % t, tag="factor_then_pa" if t == 0 else "pa%d" % t)
            gather(pa[:], b_win[t], n3_t[:])
            pb = sb.tile([P, PAIRS], F32, name="pb%d" % t)
            nc.vector.tensor_scalar(pb[:], b_win[t][:].indirect(n4_t[:]), -0.5, 0.0, ALU.mult, ALU.add)
            return pa, pb

        def put_back(t, pa, pb):
            nc.vector.tensor_tensor(b_win[t][:].indirect(n4_t[:]), pa[:], pb[:], ALU.add)
            twice = sb.tile([P, wide_hi - wide_lo], F32, name="twice%d" % t)
            nc.scalar.activation(twice[:], b_win[t][:, wide_lo:wide_hi], ACT.Copy, scale=two_column[:] if t == PACK - 1 else 2.0)
            doubled[0, t] = twice[:]

        picked = pick_pairs(0)
        for t in range(PACK):
            ahead = pick_pairs(t + 1) if t + 1 < PACK else None
            put_back(t, *picked)
            picked = ahead
        doubled_rest = sb.tile([P, PACK, N - wide_hi], F32, name="doubled_rest", tag="two_then_doubled", align_bytes=64)
        for n, (lo, hi) in list(enumerate(PIECES))[1:]:
            for t in range(PACK):
                doubled[n, t] = doubled_rest[:, t, lo - wide_hi : hi - wide_hi]
                nc.scalar.activation(doubled[n, t], b_win[t][:, lo:hi], ACT.Copy, scale=2.0)

        z_bytes = sb.tile([P, N], U8, name="z_bytes", align_bytes=64)

        def quantise_z(lo, hi, codes):
            nc.vector.quantize_mx(
                out=codes.bitcast(FP8X4), scales=z_bytes[:, P * lo : P * hi], in_=z_grouped[:, lo:hi].rearrange("p u m t -> p (u m t)")
            )

        z_first = sb.tile([P, P], U32, name="z_first", align_bytes=64)
        quantise_z(0, 1, z_first[:])

        first, last = range(len(PIECES))
        width = N // 2
        diff_first = sb.tile([P, PACK, width], F32, name="diff_first", tag="diff_then_z2", align_bytes=64)
        diff_last = sb.tile([P, PACK, width], F32, name="diff_last")
        diff = [diff_first, diff_last]
        z2_codes = [sb.tile([P, width], U32, name="z2_codes%d" % n, align_bytes=64) for n in range(len(PIECES))]
        z2_bytes = [sb.tile([P, width], U8, name="z2_bytes%d" % n, align_bytes=64) for n in range(len(PIECES))]
        s_acc = {t: psum.tile([P, N], F32, name="s_acc", tag="wide", bufs=4) for t in range(1, PACK)}

        def fetch5(n):
            lo, hi = PIECES[n]
            for t in range(PACK):
                nc.vector.tensor_tensor(
                    diff[n][:, t, :], b_win[t][:].indirect(n5_t[:, lo // 16 : hi // 16]), doubled[n, t], ALU.subtract
                )

        def quantise_z2(n, rounded, cols, tag):
            nc.vector.quantize_mx(
                out=z2_codes[n][:, cols].bitcast(FP8X4), scales=z2_bytes[n][:, cols], in_=rounded[:, cols].rearrange("p c j -> p (c j)")
            )
            acc = psum.tile([P, cols.stop - cols.start], F32, name="first_acc", tag=tag, bufs=2)
            mx_product(acc[:], z_first[:], z_bytes[:, :P], z2_codes[n][:, cols], z2_bytes[n][:, cols])
            lo = PIECES[n][0]
            nc.scalar.activation(a_win[0][:, lo + cols.start : lo + cols.stop], acc[:], ACT.Copy, scale=0.0625)

        fetch5(first)
        z2_first = sb.tile([P, width, PACK], BF16, name="z2_first", align_bytes=64)
        nc.scalar.activation(z2_first[:], diff_first[:].rearrange("p t c -> p c t"), ACT.Copy, scale=-0.5)
        fetch5(last)
        quantise_z2(first, z2_first, slice(0, width), "acc")
        z2_last = sb.tile([P, width, PACK], BF16, name="z2_last", tag="diff_then_z2", align_bytes=64)
        halves = (slice(0, P), slice(P, width))
        for cols in halves:
            nc.vector.tensor_scalar(
                z2_last[:, cols].rearrange("p (c i) t -> p c t i", i=4), diff_last[:, :, cols].rearrange("p t (c i) -> p c t i", i=4),
                -0.5, None, ALU.mult,
            )
        for cols in halves:
            quantise_z2(last, z2_last, cols, "back")
        z_others = sb.tile([P, (PACK - 1) * P], U32, name="z_others", tag="diff_then_z2", align_bytes=64)
        quantise_z(1, 2, z_others[:, :P])
        quantise_z(2, 4, z_others[:, P:])
        z_codes = [z_first[:]] + [z_others[:, P * n : P * (n + 1)] for n in range(PACK - 1)]
        sixteenth = pair[0][:, :1]
        nc.scalar.activation(sixteenth, a_win[0][:, N : N + 1], ACT.Copy, bias=0.0625)
        for t in range(1, PACK):
            for n, (lo, hi) in enumerate(PIECES):
                mx_product(s_acc[t][:, lo:hi], z_codes[t], z_bytes[:, P * t : P * (t + 1)], z2_codes[n][:], z2_bytes[n][:])

        def empty_s(t):
            nc.scalar.activation(a_win[t][:, :N], s_acc[t][:], ACT.Copy, scale=sixteenth if t == 1 else 0.0625)

        out_rows = out.rearrange("(p t) v -> t p v", t=PACK)
        hop6 = [sb.tile([P, N], F32, name="hop6_%d" % t) for t in range(PACK)]
        hop7 = [sb.tile([P, N], F32, name="hop7_%d" % t) for t in range(PACK)]
        res = [sb.tile([P, N], F32, name="res%d" % t) for t in range(PACK)]
        negated = {}

        def fetch6(t):
            gather(hop6[t][:], a_win[t], n6_t[:])

        def larger(t):
            nc.vector.tensor_tensor(pair[t][:, :N], a_win[t][:, :N], hop6[t][:], ALU.max)

        def fetch7(t, lo=0, hi=N):
            gather(hop7[t][:, lo:hi], pair[t], n7_t[:, lo // 16 : hi // 16])

        def smaller(t, lo=0, hi=N):
            nc.vector.tensor_tensor(res[t][:, lo:hi], pair[t][:, lo:hi], hop7[t][:, lo:hi], ALU.min)
            nc.sync.dma_start(out_rows[t][:, lo:hi], res[t][:, lo:hi])

        def turn(dst, terms, func, scale, tag):
            turned = psum.tile([P, N], F32, name="turned", tag=tag, bufs=2)
            for j in range(PACK):
                cols = slice(P * j, P * (j + 1))
                add_transposed(turned[:, cols], [term[:, cols] for term in terms])
            nc.scalar.activation(dst, turned[:], func, scale=scale)

        def negate(t):
            minus = sb.tile([P, N], F32, name="minus%d" % t)
            nc.scalar.activation(minus[:], pair[t][:, :N], ACT.Copy, scale=-1.0)
            minus_turned = sb.tile([P, N], F32, name="minus_turned%d" % t)
            turn(minus_turned[:], [minus[:]], ACT.Copy, 1.0, "acc")
            negated[t] = (minus, minus_turned)

        def smaller_by_transposes(t):
            minus, minus_turned = negated[t]
            over = sb.tile([P, N], F32, name="over%d" % t)
            turn(over[:], [minus[:], hop7[t][:]], ACT.Relu, -1.0, "back")
            turn(res[t][:], [minus_turned[:], over[:]], ACT.Copy, -1.0, "acc")
            nc.scalar.dma_start(out_rows[t], res[t][:])

        for t in range(1, PACK):
            empty_s(t)
        fetch6(0)
        fetch6(1)
        for t in range(2):
            larger(t)
            negate(t)
        for t in range(2):
            fetch7(t)
            smaller_by_transposes(t)
        fetch6(2)
        fetch6(3)
        larger(2)
        larger(3)
        fetch7(2)
        fetch7(3, 0, N // 2)
        smaller(2)
        fetch7(3, N // 2, N)
        smaller(3, 0, N // 2)
        smaller(3, N // 2, N)
